import numpy as np
import ml_dtypes


def mxq(x, axis, fmt="e4m3"):
    dtype, down = {"e4m3": (ml_dtypes.float8_e4m3fn, 7), "e5m2": (ml_dtypes.float8_e5m2, 14)}[fmt]
    v = np.moveaxis(np.asarray(x, np.float32).astype(ml_dtypes.bfloat16).astype(np.float64), axis, -1)
    blocks = v.reshape(v.shape[:-1] + (-1, 32))
    amax = np.abs(blocks).max(-1, keepdims=True)
    byte = np.maximum(np.where(amax > 0, np.frexp(amax)[1] - 1 + 127, 0) - down, 1)
    scale = np.exp2(byte - 127.0)
    codes = (blocks / scale).astype(np.float32).astype(dtype).astype(np.float64)
    return np.moveaxis((codes * scale).reshape(v.shape), -1, axis)


WIDE = False


def mx_kscale(k):
    if not WIDE:
        return np.ones(k)
    levels = np.array([10, -10, 5, -5, 0])
    if k % 512:
        return np.exp2(np.random.permutation(np.resize(levels, k // 32))).repeat(32)
    a = np.empty((k // 512, 16))
    for p in range(k // 512):
        a[p, :8] = np.random.permutation(np.resize(levels, 8))
        for g in range(8):
            far = levels[np.abs(levels - a[p, g]) >= 10]
            a[p, g + 8] = far[np.random.randint(len(far))]
    return np.exp2(a.ravel()).repeat(32)


def f64(x):
    return np.asarray(x).astype(np.float64)


def striped(idx):
    return np.tile(idx.reshape(-1, 16).T, (8, 1)).astype(np.uint16)


def unstriped(offs):
    return offs[:16].T.reshape(-1).astype(np.int64)


def relu(v):
    return np.maximum(v, 0.0)


def sigmoid(v):
    return 1.0 / (1.0 + np.exp(-np.maximum(v, -700.0)))


K, T, S, V, N = 512, 4096, 1024, 512, 256


def setup_inputs():
    n = np.random.standard_normal
    s = mx_kscale(K)[:, None]
    return {
        "xT": (n((K, T)) * s).astype(np.float32),
        "w1": (n((K, N)) / np.sqrt(K) / s).astype(np.float32),
        "w2": (n((K, N)) / np.sqrt(K) / s).astype(np.float32),
        "w3": (n((K, N)) / np.sqrt(K) / s).astype(np.float32),
        "offs": striped(np.random.permutation(T)[:S]),
        "cen": striped(np.random.permutation(S)[:V]),
        "pos1": striped(np.random.permutation(S)[:V]),
        "pos2": striped(np.random.permutation(S)[:V]),
    }


def reference(xT, w1, w2, w3, offs, cen, pos1, pos2):
    xq = mxq(f64(xT)[:, unstriped(offs)], 0, "e4m3")
    y = mxq(f64(w1), 0, "e4m3").T @ xq
    yc = y[:, unstriped(cen)]
    e = mxq(f64(w2), 0, "e4m3").T @ xq
    h = mxq(f64(w3), 0, "e4m3").T @ xq
    z = (sigmoid(yc + e[:, unstriped(pos1)])) * h[:, unstriped(pos1)] + (sigmoid(yc + e[:, unstriped(pos2)])) * h[:, unstriped(pos2)]
    return relu(z)

@@ -1,0 +1,179 @@
+from contextlib import ExitStack
+
+import concourse.mybir as mybir
+
+K, T, S, V, N = 512, 4096, 1024, 512, 256
+FLOPS = 3 * 2 * K * N * S
+
+F32 = mybir.dt.float32
+BF16 = mybir.dt.bfloat16
+U32 = mybir.dt.uint32
+U16 = mybir.dt.uint16
+U8 = mybir.dt.uint8
+FP8X4 = mybir.dt.float8_e4m3fn_x4
+ACT = mybir.ActivationFunctionType
+ALU = mybir.AluOpType
+
+P = 128
+HALF = S // 2
+CHUNKS = ((1024, 1024, 1024, 1024), (1024, 1024, 1024, 512, 256, 256))
+PIECES = ((0, 512), (512, 768), (768, 1024))
+
+
+def tile_picked_gatedg_relu_e_kernel(tc, xT, w1, w2, w3, offs, cen, pos1, pos2, out):
+    nc = tc.nc
+    with ExitStack() as ctx:
+        keep = ctx.enter_context(tc.tile_pool(name="keep", bufs=1))
+        psum = ctx.enter_context(tc.psum_pool(name="psum", bufs=4))
+
+        warm_in = keep.tile([P, 8], F32, name="warm_in")
+        warm_out = keep.tile([P, 8], F32, name="warm_out")
+        nc.vector.memset(warm_in[:], 0.0)
+        nc.scalar.activation(warm_out[:], warm_in[:], ACT.Sigmoid)
+
+        def load_list(src, name):
+            lst = keep.tile(list(src.shape), U16, name=name)
+            nc.sync.dma_start(lst[:], src)
+            return lst
+
+        def load_weight(w, name):
+            raw = keep.tile([P, 4, N], F32, name=name + "_raw")
+            nc.sync.dma_start(raw[:], w.rearrange("(p j) n -> p j n", j=4))
+            return raw
+
+        def round_weight(copy, raw, name, tag):
+            grouped = keep.tile([P, N * 4], BF16, name=name + "_bf", tag=tag, align_bytes=64)
+            copy(
+                grouped[:].rearrange("p (c i j) -> p c j i", i=4, j=4),
+                raw[:].rearrange("p j (c i) -> p c j i", i=4),
+            )
+            return grouped
+
+        def quantize(grouped, width, name):
+            codes = keep.tile([P, width], U32, name=name + "_codes", align_bytes=64)
+            scales = keep.tile([P, width], U8, name=name + "_scales", align_bytes=64)
+            nc.vector.quantize_mx(out=codes[:].bitcast(FP8X4), scales=scales[:], in_=grouped)
+            return codes, scales
+
+        x_rows = xT.rearrange("(p u e) t -> p u e t", u=2, e=2)
+        pairs = [keep.tile([P, 2 * T], BF16, name="pairs%d" % u) for u in range(2)]
+        picked = [keep.tile([P, 2, HALF], U32, name="picked%d" % a) for a in range(2)]
+
+        def load_chunks(u):
+            raws, c0 = [], 0
+            for width in CHUNKS[u]:
+                raw = keep.tile([P, 2, width], F32, name="x_raw%d_%d" % (u, c0))
+                nc.sync.dma_start(raw[:], x_rows[:, u, :, c0 : c0 + width])
+                raws.append((raw, c0, width))
+                c0 = c0 + width
+            return raws
+
+        def round_chunk(copy, u, raw, c0, width):
+            copy(
+                pairs[u][:, 2 * c0 : 2 * (c0 + width)].rearrange("p (c i e) -> p c e i", i=4, e=2),
+                raw[:].rearrange("p e (c i) -> p c e i", i=4),
+            )
+
+        def gather_pairs(u):
+            for a in range(2):
+                nc.vector.tensor_copy(
+                    picked[a][:, u, :],
+                    pairs[u][:].bitcast(U32).indirect(offs_t[:, a * HALF // 16 : (a + 1) * HALF // 16]),
+                )
+
+        raws0 = load_chunks(0)
+        offs_t = load_list(offs, "offs_t")
+        w1_raw = load_weight(w1, "w1")
+        raws1 = load_chunks(1)
+        w2_raw = load_weight(w2, "w2")
+        cen_t = load_list(cen, "cen_t")
+        pos_t = [load_list(pos1, "pos1_t"), load_list(pos2, "pos2_t")]
+        w3_raw = load_weight(w3, "w3")
+
+        for raw, c0, width in raws0:
+            round_chunk(nc.vector.tensor_copy, 0, raw, c0, width)
+        gather_pairs(0)
+        w1_q = quantize(round_weight(nc.scalar.copy, w1_raw, "w1", "w1_bf")[:], N, "w1")
+        for i, (raw, c0, width) in enumerate(raws1):
+            round_chunk(nc.scalar.copy if i == 0 else nc.vector.tensor_copy, 1, raw, c0, width)
+        gather_pairs(1)
+
+        x_q = []
+        for c0, c1 in PIECES:
+            a, width = c0 // HALF, c1 - c0
+            grouped = keep.tile([P, 4 * width], BF16, name="x_bf%d" % c0, tag="x_bf%d" % c0, align_bytes=64)
+            nc.scalar.copy(
+                grouped[:].bitcast(U32).rearrange("p (n u) -> p n u", u=2),
+                picked[a][:, :, c0 - a * HALF : c1 - a * HALF].rearrange("p u n -> p n u"),
+            )
+            x_q.append(quantize(grouped[:], width, "x%d" % c0))
+        w2_q = quantize(round_weight(nc.vector.tensor_copy, w2_raw, "w2", "x_bf0")[:], N, "w2")
+        w3_q = quantize(round_weight(nc.scalar.copy, w3_raw, "w3", "w3_bf")[:], N, "w3")
+
+        def product(w_q, b, name, second_copy):
+            rows = keep.tile([P, S], F32, name=name)
+            cols = slice(b * P, (b + 1) * P)
+            for a, copy in ((0, nc.scalar.copy), (1, second_copy)):
+                acc = psum.tile([P, HALF], F32, name="acc")
+                for (c0, c1), (codes, scales) in zip(PIECES, x_q):
+                    if c0 // HALF == a:
+                        nc.tensor.matmul_mx(
+                            out=acc[:, c0 - a * HALF : c1 - a * HALF],
+                            lhsT=w_q[0][:, cols].bitcast(FP8X4),
+                            lhsT_scale=w_q[1][:, cols],
+                            rhs=codes[:].bitcast(FP8X4),
+                            rhs_scale=scales[:],
+                            start=True,
+                            stop=True,
+                        )
+                copy(rows[:, a * HALF : (a + 1) * HALF], acc[:])
+            return rows
+
+        def sums(b, y, e):
+            yc = keep.tile([P, V], F32, name="yc%d" % b)
+            nc.vector.tensor_copy(yc[:], y[:].indirect(cen_t[:]))
+            res = []
+            for d in range(2):
+                pre = keep.tile([P, V], F32, name="pre%d_%d" % (b, d))
+                nc.vector.tensor_tensor(pre[:], e[:].indirect(pos_t[d][:]), yc[:], ALU.add)
+                res.append(pre)
+            return res
+
+        def sigmoid(pre, name):
+            gate = keep.tile([P, V], F32, name=name)
+            nc.scalar.activation(gate[:], pre[:], ACT.Sigmoid)
+            return gate
+
+        def message(h, gate, d, name):
+            msg = keep.tile([P, V], F32, name=name)
+            nc.vector.tensor_tensor(msg[:], h[:].indirect(pos_t[d][:]), gate[:], ALU.mult)
+            return msg
+
+        def finish(b, msg, parts):
+            width = V // parts
+            for i in range(parts):
+                cols = slice(i * width, (i + 1) * width)
+                total = keep.tile([P, width], F32, name="total%d_%d" % (b, i))
+                nc.vector.tensor_tensor(total[:], msg[0][:, cols], msg[1][:, cols], ALU.add)
+                res = keep.tile([P, width], F32, name="res%d_%d" % (b, i))
+                nc.scalar.activation(res[:], total[:], ACT.Relu)
+                nc.sync.dma_start(out[b * P : (b + 1) * P, cols], res[:])
+
+        y0 = product(w1_q, 0, "y0", nc.vector.tensor_copy)
+        e0 = product(w2_q, 0, "e0", nc.scalar.copy)
+        pre0 = sums(0, y0, e0)
+        y1 = product(w1_q, 1, "y1", nc.scalar.copy)
+        e1 = product(w2_q, 1, "e1", nc.scalar.copy)
+        pre1 = sums(1, y1, e1)
+        g00 = sigmoid(pre0[0], "gate00")
+        h0 = product(w3_q, 0, "h0", nc.scalar.copy)
+        g01 = sigmoid(pre0[1], "gate01")
+        h1 = product(w3_q, 1, "h1", nc.scalar.copy)
+        g10 = sigmoid(pre1[0], "gate10")
+        g11 = sigmoid(pre1[1], "gate11")
+        m00 = message(h0, g00, 0, "msg00")
+        m01 = message(h0, g01, 1, "msg01")
+        m10 = message(h1, g10, 0, "msg10")
+        finish(0, [m00, m01], 1)
+        m11 = message(h1, g11, 1, "msg11")
+        finish(1, [m10, m11], 2)

@@ -8,6 +8,7 @@ FLOPS = 3 * 2 * K * N * S
 F32 = mybir.dt.float32
 BF16 = mybir.dt.bfloat16
 U32 = mybir.dt.uint32
+I32 = mybir.dt.int32
 U16 = mybir.dt.uint16
 U8 = mybir.dt.uint8
 FP8X4 = mybir.dt.float8_e4m3fn_x4
@@ -16,7 +17,7 @@ ALU = mybir.AluOpType
 
 P = 128
 HALF = S // 2
-CHUNKS = ((1024, 1024, 1024, 1024), (1024, 1024, 1024, 512, 256, 256))
+CHUNKS = ((2048, 2048), (2048, 1024, 512, 256, 256))
 PIECES = ((0, 512), (512, 768), (768, 1024))
 
 
@@ -24,7 +25,7 @@ def tile_picked_gatedg_relu_e_kernel(tc, xT, w1, w2, w3, offs, cen, pos1, pos2, 
     nc = tc.nc
     with ExitStack() as ctx:
         keep = ctx.enter_context(tc.tile_pool(name="keep", bufs=1))
-        psum = ctx.enter_context(tc.psum_pool(name="psum", bufs=4))
+        psum = ctx.enter_context(tc.psum_pool(name="psum", bufs=1))
 
         warm_in = keep.tile([P, 8], F32, name="warm_in")
         warm_out = keep.tile([P, 8], F32, name="warm_out")
@@ -37,42 +38,45 @@ def tile_picked_gatedg_relu_e_kernel(tc, xT, w1, w2, w3, offs, cen, pos1, pos2, 
             return lst
 
         def load_weight(w, name):
-            raw = keep.tile([P, 4, N], F32, name=name + "_raw")
+            raw = keep.tile([P, 4, N], F32, name=name + "_raw", tag=name + "_raw", align_bytes=256)
             nc.sync.dma_start(raw[:], w.rearrange("(p j) n -> p j n", j=4))
             return raw
 
-        def round_weight(copy, raw, name, tag):
-            grouped = keep.tile([P, N * 4], BF16, name=name + "_bf", tag=tag, align_bytes=64)
-            copy(
+        def round_weight(raw, c0, c1, name, tag):
+            grouped = keep.tile([P, (c1 - c0) * 4], BF16, name=name + "_bf", tag=tag, align_bytes=256)
+            nc.scalar.copy(
                 grouped[:].rearrange("p (c i j) -> p c j i", i=4, j=4),
-                raw[:].rearrange("p j (c i) -> p c j i", i=4),
+                raw[:, :, c0:c1].rearrange("p j (c i) -> p c j i", i=4),
             )
             return grouped
 
-        def quantize(grouped, width, name):
-            codes = keep.tile([P, width], U32, name=name + "_codes", align_bytes=64)
+        def quantize(grouped, width, name, tag):
+            codes = keep.tile([P, width], U32, name=name + "_codes", tag=tag, align_bytes=256)
             scales = keep.tile([P, width], U8, name=name + "_scales", align_bytes=64)
             nc.vector.quantize_mx(out=codes[:].bitcast(FP8X4), scales=scales[:], in_=grouped)
             return codes, scales
 
         x_rows = xT.rearrange("(p u e) t -> p u e t", u=2, e=2)
         pairs = [keep.tile([P, 2 * T], BF16, name="pairs%d" % u) for u in range(2)]
-        picked = [keep.tile([P, 2, HALF], U32, name="picked%d" % a) for a in range(2)]
+        picked = [keep.tile([P, 2, HALF], U32, name="picked%d" % a, tag="picked%d" % a, align_bytes=256) for a in range(2)]
 
         def load_chunks(u):
             raws, c0 = [], 0
             for width in CHUNKS[u]:
-                raw = keep.tile([P, 2, width], F32, name="x_raw%d_%d" % (u, c0))
+                raw = keep.tile([P, 2, width], F32, name="x_raw%d_%d" % (u, c0), align_bytes=256)
                 nc.sync.dma_start(raw[:], x_rows[:, u, :, c0 : c0 + width])
                 raws.append((raw, c0, width))
                 c0 = c0 + width
             return raws
 
-        def round_chunk(copy, u, raw, c0, width):
-            copy(
-                pairs[u][:, 2 * c0 : 2 * (c0 + width)].rearrange("p (c i e) -> p c e i", i=4, e=2),
-                raw[:].rearrange("p e (c i) -> p c e i", i=4),
-            )
+        def round_chunk(u, raw, c0, width):
+            cut = width * 11 // 16
+            shares = ((nc.vector.tensor_copy, 0, cut), (nc.scalar.copy, cut, width))
+            for copy, a, b in shares if width > 256 else ((nc.vector.tensor_copy, 0, width),):
+                copy(
+                    pairs[u][:, 2 * (c0 + a) : 2 * (c0 + b)].rearrange("p (c i e) -> p c e i", i=4, e=2),
+                    raw[:, :, a:b].rearrange("p e (c i) -> p c e i", i=4),
+                )
 
         def gather_pairs(u):
             for a in range(2):
@@ -83,38 +87,44 @@ def tile_picked_gatedg_relu_e_kernel(tc, xT, w1, w2, w3, offs, cen, pos1, pos2, 
 
         raws0 = load_chunks(0)
         offs_t = load_list(offs, "offs_t")
-        w1_raw = load_weight(w1, "w1")
         raws1 = load_chunks(1)
+        w1_raw = load_weight(w1, "w1")
         w2_raw = load_weight(w2, "w2")
         cen_t = load_list(cen, "cen_t")
         pos_t = [load_list(pos1, "pos1_t"), load_list(pos2, "pos2_t")]
         w3_raw = load_weight(w3, "w3")
 
-        for raw, c0, width in raws0:
-            round_chunk(nc.vector.tensor_copy, 0, raw, c0, width)
-        gather_pairs(0)
-        w1_q = quantize(round_weight(nc.scalar.copy, w1_raw, "w1", "w1_bf")[:], N, "w1")
-        for i, (raw, c0, width) in enumerate(raws1):
-            round_chunk(nc.scalar.copy if i == 0 else nc.vector.tensor_copy, 1, raw, c0, width)
-        gather_pairs(1)
+        for u, raws in enumerate((raws0, raws1)):
+            for raw, c0, width in raws:
+                round_chunk(u, raw, c0, width)
+            gather_pairs(u)
 
-        x_q = []
-        for c0, c1 in PIECES:
-            a, width = c0 // HALF, c1 - c0
-            grouped = keep.tile([P, 4 * width], BF16, name="x_bf%d" % c0, tag="x_bf%d" % c0, align_bytes=64)
-            nc.scalar.copy(
-                grouped[:].bitcast(U32).rearrange("p (n u) -> p n u", u=2),
-                picked[a][:, :, c0 - a * HALF : c1 - a * HALF].rearrange("p u n -> p n u"),
+        def weave(copy, word, grouped, a, c0, c1):
+            copy(
+                grouped[:, 4 * c0 : 4 * c1].bitcast(word).rearrange("p (n u) -> p n u", u=2),
+                picked[a][:, :, c0:c1].bitcast(word).rearrange("p u n -> p n u"),
             )
-            x_q.append(quantize(grouped[:], width, "x%d" % c0))
-        w2_q = quantize(round_weight(nc.vector.tensor_copy, w2_raw, "w2", "x_bf0")[:], N, "w2")
-        w3_q = quantize(round_weight(nc.scalar.copy, w3_raw, "w3", "w3_bf")[:], N, "w3")
 
-        def product(w_q, b, name, second_copy):
-            rows = keep.tile([P, S], F32, name=name)
+        w1_bf = round_weight(w1_raw, 0, N, "w1", "w1_bf")
+        w2_bf = round_weight(w2_raw, 0, N, "w2", "w2_bf")
+        x_bf0 = keep.tile([P, 4 * HALF], BF16, name="x_bf0", align_bytes=256)
+        x_bf1 = keep.tile([P, 4 * HALF], BF16, name="x_bf1", tag="w2_raw", align_bytes=256)
+        weave(nc.vector.tensor_copy, I32, x_bf0, 0, 0, 512)
+        weave(nc.scalar.copy, U32, x_bf1, 1, 0, 256)
+        weave(nc.scalar.copy, U32, x_bf1, 1, 256, 512)
+        w1_q = quantize(w1_bf[:], N, "w1", "w1_codes")
+        x_q = [
+            quantize(x_bf0[:], 512, "x0", "w1_bf"),
+            quantize(x_bf1[:, 0:1024], 256, "x512", "x512_codes"),
+            quantize(x_bf1[:, 1024:2048], 256, "x768", "x768_codes"),
+        ]
+        w2_q = quantize(w2_bf[:], N, "w2", "w2_raw")
+
+        def product(w_q, b, name, second_copy, bank):
+            rows = keep.tile([P, S], F32, name=name, tag=name, align_bytes=256)
             cols = slice(b * P, (b + 1) * P)
             for a, copy in ((0, nc.scalar.copy), (1, second_copy)):
-                acc = psum.tile([P, HALF], F32, name="acc")
+                acc = psum.tile([P, HALF], F32, name="acc", tag="bank%d" % ((bank + a) % 3))
                 for (c0, c1), (codes, scales) in zip(PIECES, x_q):
                     if c0 // HALF == a:
                         nc.tensor.matmul_mx(
@@ -140,40 +150,50 @@ def tile_picked_gatedg_relu_e_kernel(tc, xT, w1, w2, w3, offs, cen, pos1, pos2, 
             return res
 
         def sigmoid(pre, name):
-            gate = keep.tile([P, V], F32, name=name)
+            gate = keep.tile([P, V], F32, name=name, tag=name)
             nc.scalar.activation(gate[:], pre[:], ACT.Sigmoid)
             return gate
 
-        def message(h, gate, d, name):
+        def message(h, gate, d, name, parts=1):
             msg = keep.tile([P, V], F32, name=name)
-            nc.vector.tensor_tensor(msg[:], h[:].indirect(pos_t[d][:]), gate[:], ALU.mult)
+            width = V // parts
+            for i in range(parts):
+                cols = slice(i * width, (i + 1) * width)
+                entries = pos_t[d][:, i * width // 16 : (i + 1) * width // 16]
+                nc.vector.tensor_tensor(msg[:, cols], h[:].indirect(entries), gate[:, cols], ALU.mult)
             return msg
 
         def finish(b, msg, parts):
             width = V // parts
             for i in range(parts):
                 cols = slice(i * width, (i + 1) * width)
-                total = keep.tile([P, width], F32, name="total%d_%d" % (b, i))
+                tag = "gate10" if b == 0 else "total%d" % i
+                total = keep.tile([P, width], F32, name="total%d_%d" % (b, i), tag=tag)
                 nc.vector.tensor_tensor(total[:], msg[0][:, cols], msg[1][:, cols], ALU.add)
                 res = keep.tile([P, width], F32, name="res%d_%d" % (b, i))
-                nc.scalar.activation(res[:], total[:], ACT.Relu)
+                if i == 1:
+                    nc.vector.tensor_scalar_max(res[:], total[:], 0.0)
+                else:
+                    nc.scalar.activation(res[:], total[:], ACT.Relu)
                 nc.sync.dma_start(out[b * P : (b + 1) * P, cols], res[:])
 
-        y0 = product(w1_q, 0, "y0", nc.vector.tensor_copy)
-        e0 = product(w2_q, 0, "e0", nc.scalar.copy)
+        y0 = product(w1_q, 0, "y0", nc.vector.tensor_copy, 0)
+        e0 = product(w2_q, 0, "e0", nc.scalar.copy, 2)
+        w3a_q = quantize(round_weight(w3_raw, 0, P, "w3a", "picked1")[:], P, "w3a", "w3a_codes")
         pre0 = sums(0, y0, e0)
-        y1 = product(w1_q, 1, "y1", nc.scalar.copy)
-        e1 = product(w2_q, 1, "e1", nc.scalar.copy)
+        y1 = product(w1_q, 1, "y1", nc.scalar.copy, 4)
+        w3b_q = quantize(round_weight(w3_raw, P, N, "w3b", "w1_codes")[:], P, "w3b", "w3b_codes")
+        e1 = product(w2_q, 1, "e1", nc.scalar.copy, 6)
         pre1 = sums(1, y1, e1)
         g00 = sigmoid(pre0[0], "gate00")
-        h0 = product(w3_q, 0, "h0", nc.scalar.copy)
         g01 = sigmoid(pre0[1], "gate01")
-        h1 = product(w3_q, 1, "h1", nc.scalar.copy)
+        h0 = product(w3a_q, 0, "h0", nc.scalar.copy, 8)
+        h1 = product(w3b_q, 0, "h1", nc.scalar.copy, 10)
         g10 = sigmoid(pre1[0], "gate10")
         g11 = sigmoid(pre1[1], "gate11")
         m00 = message(h0, g00, 0, "msg00")
         m01 = message(h0, g01, 1, "msg01")
         m10 = message(h1, g10, 0, "msg10")
         finish(0, [m00, m01], 1)
-        m11 = message(h1, g11, 1, "msg11")
+        m11 = message(h1, g11, 1, "msg11", 2)
         finish(1, [m10, m11], 2)

@@ -8,7 +8,6 @@ FLOPS = 3 * 2 * K * N * S
 F32 = mybir.dt.float32
 BF16 = mybir.dt.bfloat16
 U32 = mybir.dt.uint32
-I32 = mybir.dt.int32
 U16 = mybir.dt.uint16
 U8 = mybir.dt.uint8
 FP8X4 = mybir.dt.float8_e4m3fn_x4
@@ -18,7 +17,6 @@ ALU = mybir.AluOpType
 P = 128
 HALF = S // 2
 CHUNKS = ((2048, 2048), (2048, 1024, 512, 256, 256))
-PIECES = ((0, 512), (512, 768), (768, 1024))
 
 
 def tile_picked_gatedg_relu_e_kernel(tc, xT, w1, w2, w3, offs, cen, pos1, pos2, out):
@@ -58,7 +56,8 @@ def tile_picked_gatedg_relu_e_kernel(tc, xT, w1, w2, w3, offs, cen, pos1, pos2, 
 
         x_rows = xT.rearrange("(p u e) t -> p u e t", u=2, e=2)
         pairs = [keep.tile([P, 2 * T], BF16, name="pairs%d" % u) for u in range(2)]
-        picked = [keep.tile([P, 2, HALF], U32, name="picked%d" % a, tag="picked%d" % a, align_bytes=256) for a in range(2)]
+        picked = keep.tile([P, 2, HALF], U32, name="picked", tag="picked", align_bytes=256)
+        x_bf1 = keep.tile([P, 4 * HALF], BF16, name="x_bf1", tag="x_bf1", align_bytes=256)
 
         def load_chunks(u):
             raws, c0 = [], 0
@@ -79,11 +78,12 @@ def tile_picked_gatedg_relu_e_kernel(tc, xT, w1, w2, w3, offs, cen, pos1, pos2, 
                 )
 
         def gather_pairs(u):
-            for a in range(2):
-                nc.vector.tensor_copy(
-                    picked[a][:, u, :],
-                    pairs[u][:].bitcast(U32).indirect(offs_t[:, a * HALF // 16 : (a + 1) * HALF // 16]),
-                )
+            window = pairs[u][:].bitcast(U32)
+            nc.vector.tensor_copy(picked[:, u, :], window.indirect(offs_t[:, 0 : HALF // 16]))
+            nc.vector.tensor_copy(
+                x_bf1[:].bitcast(U32).rearrange("p (n u) -> p n u", u=2)[:, :, u],
+                window.indirect(offs_t[:, HALF // 16 : S // 16]),
+            )
 
         raws0 = load_chunks(0)
         offs_t = load_list(offs, "offs_t")
@@ -99,49 +99,44 @@ def tile_picked_gatedg_relu_e_kernel(tc, xT, w1, w2, w3, offs, cen, pos1, pos2, 
                 round_chunk(u, raw, c0, width)
             gather_pairs(u)
 
-        def weave(copy, word, grouped, a, c0, c1):
-            copy(
-                grouped[:, 4 * c0 : 4 * c1].bitcast(word).rearrange("p (n u) -> p n u", u=2),
-                picked[a][:, :, c0:c1].bitcast(word).rearrange("p u n -> p n u"),
-            )
-
         w1_bf = round_weight(w1_raw, 0, N, "w1", "w1_bf")
-        w2_bf = round_weight(w2_raw, 0, N, "w2", "w2_bf")
-        x_bf0 = keep.tile([P, 4 * HALF], BF16, name="x_bf0", align_bytes=256)
-        x_bf1 = keep.tile([P, 4 * HALF], BF16, name="x_bf1", tag="w2_raw", align_bytes=256)
-        weave(nc.vector.tensor_copy, I32, x_bf0, 0, 0, 512)
-        weave(nc.scalar.copy, U32, x_bf1, 1, 0, 256)
-        weave(nc.scalar.copy, U32, x_bf1, 1, 256, 512)
+        x_bf0 = keep.tile([P, 4 * HALF], BF16, name="x_bf0", tag="w1_raw", align_bytes=256)
+        nc.scalar.copy(
+            x_bf0[:].bitcast(U32).rearrange("p (n u) -> p n u", u=2),
+            picked[:].rearrange("p u n -> p n u"),
+        )
+        w2_bf = round_weight(w2_raw, 0, N, "w2", "picked")
         w1_q = quantize(w1_bf[:], N, "w1", "w1_codes")
         x_q = [
-            quantize(x_bf0[:], 512, "x0", "w1_bf"),
-            quantize(x_bf1[:, 0:1024], 256, "x512", "x512_codes"),
-            quantize(x_bf1[:, 1024:2048], 256, "x768", "x768_codes"),
-        ]
-        w2_q = quantize(w2_bf[:], N, "w2", "w2_raw")
+            quantize(x_bf1[:], HALF, "x1", "w1_bf"),
+            quantize(x_bf0[:], HALF, "x0", "x0_codes"),
+        ][::-1]
+        w2_q = quantize(w2_bf[:], N, "w2", "w2_codes")
 
-        def product(w_q, b, name, second_copy, bank):
-            rows = keep.tile([P, S], F32, name=name, tag=name, align_bytes=256)
+        def product(w_q, b, name, bank, first_copy=nc.scalar.copy, order=(0, 1)):
+            rows = keep.tile([P, S], F32, name=name, tag="w1_raw" if name == "y0" else name, align_bytes=256)
             cols = slice(b * P, (b + 1) * P)
-            for a, copy in ((0, nc.scalar.copy), (1, second_copy)):
-                acc = psum.tile([P, HALF], F32, name="acc", tag="bank%d" % ((bank + a) % 3))
-                for (c0, c1), (codes, scales) in zip(PIECES, x_q):
-                    if c0 // HALF == a:
-                        nc.tensor.matmul_mx(
-                            out=acc[:, c0 - a * HALF : c1 - a * HALF],
-                            lhsT=w_q[0][:, cols].bitcast(FP8X4),
-                            lhsT_scale=w_q[1][:, cols],
-                            rhs=codes[:].bitcast(FP8X4),
-                            rhs_scale=scales[:],
-                            start=True,
-                            stop=True,
-                        )
+            for i, a in enumerate(order):
+                copy = first_copy if i == 0 else nc.scalar.copy
+                acc = psum.tile([P, HALF], F32, name="acc", tag="bank%d" % ((bank + i) % 3))
+                nc.tensor.matmul_mx(
+                    out=acc[:],
+                    lhsT=w_q[0][:, cols].bitcast(FP8X4),
+                    lhsT_scale=w_q[1][:, cols],
+                    rhs=x_q[a][0][:].bitcast(FP8X4),
+                    rhs_scale=x_q[a][1][:],
+                    start=True,
+                    stop=True,
+                )
                 copy(rows[:, a * HALF : (a + 1) * HALF], acc[:])
             return rows
 
-        def sums(b, y, e):
-            yc = keep.tile([P, V], F32, name="yc%d" % b)
+        def centres(y, name):
+            yc = keep.tile([P, V], F32, name=name)
             nc.vector.tensor_copy(yc[:], y[:].indirect(cen_t[:]))
+            return yc
+
+        def sums(b, yc, e):
             res = []
             for d in range(2):
                 pre = keep.tile([P, V], F32, name="pre%d_%d" % (b, d))
@@ -165,30 +160,34 @@ def tile_picked_gatedg_relu_e_kernel(tc, xT, w1, w2, w3, offs, cen, pos1, pos2, 
 
         def finish(b, msg, parts):
             width = V // parts
+            totals = []
             for i in range(parts):
                 cols = slice(i * width, (i + 1) * width)
                 tag = "gate10" if b == 0 else "total%d" % i
                 total = keep.tile([P, width], F32, name="total%d_%d" % (b, i), tag=tag)
                 nc.vector.tensor_tensor(total[:], msg[0][:, cols], msg[1][:, cols], ALU.add)
+                totals.append(total)
+            for i, total in enumerate(totals):
                 res = keep.tile([P, width], F32, name="res%d_%d" % (b, i))
-                if i == 1:
+                if b == 1:
                     nc.vector.tensor_scalar_max(res[:], total[:], 0.0)
                 else:
                     nc.scalar.activation(res[:], total[:], ACT.Relu)
-                nc.sync.dma_start(out[b * P : (b + 1) * P, cols], res[:])
+                nc.sync.dma_start(out[b * P : (b + 1) * P, i * width : (i + 1) * width], res[:])
 
-        y0 = product(w1_q, 0, "y0", nc.vector.tensor_copy, 0)
-        e0 = product(w2_q, 0, "e0", nc.scalar.copy, 2)
-        w3a_q = quantize(round_weight(w3_raw, 0, P, "w3a", "picked1")[:], P, "w3a", "w3a_codes")
-        pre0 = sums(0, y0, e0)
-        y1 = product(w1_q, 1, "y1", nc.scalar.copy, 4)
-        w3b_q = quantize(round_weight(w3_raw, P, N, "w3b", "w1_codes")[:], P, "w3b", "w3b_codes")
-        e1 = product(w2_q, 1, "e1", nc.scalar.copy, 6)
-        pre1 = sums(1, y1, e1)
+        y0 = product(w1_q, 0, "y0", 0, first_copy=nc.vector.tensor_copy, order=(1, 0))
+        yc0 = centres(y0, "yc0")
+        y1 = product(w1_q, 1, "y1", 2)
+        yc1 = centres(y1, "yc1")
+        e0 = product(w2_q, 0, "e0", 4)
+        pre0 = sums(0, yc0, e0)
+        w3_q = quantize(round_weight(w3_raw, 0, N, "w3", "y1")[:], N, "w3", "w3_codes")
+        e1 = product(w2_q, 1, "e1", 6)
+        pre1 = sums(1, yc1, e1)
         g00 = sigmoid(pre0[0], "gate00")
         g01 = sigmoid(pre0[1], "gate01")
-        h0 = product(w3a_q, 0, "h0", nc.scalar.copy, 8)
-        h1 = product(w3b_q, 0, "h1", nc.scalar.copy, 10)
+        h0 = product(w3_q, 0, "h0", 8)
+        h1 = product(w3_q, 1, "h1", 10)
         g10 = sigmoid(pre1[0], "gate10")
         g11 = sigmoid(pre1[1], "gate11")
         m00 = message(h0, g00, 0, "msg00")

@@ -16,7 +16,14 @@ ALU = mybir.AluOpType
 
 P = 128
 HALF = S // 2
-CHUNKS = ((2048, 2048), (2048, 1024, 512, 256, 256))
+PER_COLUMN = 16
+RUN = 4
+ALIGN = 256
+
+LOADS = ((2048, 2048), (2048, 1024, 512, 256, 256))
+VECTOR_EIGHTHS = 5
+UNSHARED_WIDTH = 256
+RING = 3
 
 
 def tile_picked_gatedg_relu_e_kernel(tc, xT, w1, w2, w3, offs, cen, pos1, pos2, out):
@@ -31,118 +38,129 @@ def tile_picked_gatedg_relu_e_kernel(tc, xT, w1, w2, w3, offs, cen, pos1, pos2, 
         nc.scalar.activation(warm_out[:], warm_in[:], ACT.Sigmoid)
 
         def load_list(src, name):
-            lst = keep.tile(list(src.shape), U16, name=name)
-            nc.sync.dma_start(lst[:], src)
-            return lst
+            entries = keep.tile(list(src.shape), U16, name=name)
+            nc.sync.dma_start(entries[:], src)
+            return entries
 
         def load_weight(w, name):
-            raw = keep.tile([P, 4, N], F32, name=name + "_raw", tag=name + "_raw", align_bytes=256)
+            raw = keep.tile([P, 4, N], F32, name=name, tag=name, align_bytes=ALIGN)
             nc.sync.dma_start(raw[:], w.rearrange("(p j) n -> p j n", j=4))
             return raw
 
-        def round_weight(raw, c0, c1, name, tag):
-            grouped = keep.tile([P, (c1 - c0) * 4], BF16, name=name + "_bf", tag=tag, align_bytes=256)
+        def round_weight(raw, name, tag):
+            grouped = keep.tile([P, N * 4], BF16, name=name, tag=tag, align_bytes=ALIGN)
             nc.scalar.copy(
-                grouped[:].rearrange("p (c i j) -> p c j i", i=4, j=4),
-                raw[:, :, c0:c1].rearrange("p j (c i) -> p c j i", i=4),
+                grouped[:].rearrange("p (c i j) -> p c j i", i=RUN, j=4),
+                raw[:].rearrange("p j (c i) -> p c j i", i=RUN),
             )
             return grouped
 
-        def quantize(grouped, width, name, tag):
-            codes = keep.tile([P, width], U32, name=name + "_codes", tag=tag, align_bytes=256)
+        def quantize(grouped, width, name, tag, parts=1):
+            codes = keep.tile([P, width], U32, name=name + "_codes", tag=tag, align_bytes=ALIGN)
             scales = keep.tile([P, width], U8, name=name + "_scales", align_bytes=64)
-            nc.vector.quantize_mx(out=codes[:].bitcast(FP8X4), scales=scales[:], in_=grouped)
+            step = width // parts
+            for c0 in range(0, width, step):
+                nc.vector.quantize_mx(
+                    out=codes[:, c0 : c0 + step].bitcast(FP8X4),
+                    scales=scales[:, c0 : c0 + step],
+                    in_=grouped[:, 4 * c0 : 4 * (c0 + step)],
+                )
             return codes, scales
 
         x_rows = xT.rearrange("(p u e) t -> p u e t", u=2, e=2)
         pairs = [keep.tile([P, 2 * T], BF16, name="pairs%d" % u) for u in range(2)]
-        picked = keep.tile([P, 2, HALF], U32, name="picked", tag="picked", align_bytes=256)
-        x_bf1 = keep.tile([P, 4 * HALF], BF16, name="x_bf1", tag="x_bf1", align_bytes=256)
+        picked = keep.tile([P, 2, HALF], U32, name="picked", tag="picked", align_bytes=ALIGN)
+        x_second = keep.tile([P, 4 * HALF], BF16, name="x_second", align_bytes=ALIGN)
 
-        def load_chunks(u):
-            raws, c0 = [], 0
-            for width in CHUNKS[u]:
-                raw = keep.tile([P, 2, width], F32, name="x_raw%d_%d" % (u, c0), align_bytes=256)
+        def load_pair(u):
+            loads, c0 = [], 0
+            for width in LOADS[u]:
+                raw = keep.tile([P, 2, width], F32, name="x_raw%d_%d" % (u, c0), align_bytes=ALIGN)
                 nc.sync.dma_start(raw[:], x_rows[:, u, :, c0 : c0 + width])
-                raws.append((raw, c0, width))
+                loads.append((raw, c0, width))
                 c0 = c0 + width
-            return raws
+            return loads
 
-        def round_chunk(u, raw, c0, width):
-            cut = width * 11 // 16
+        def round_load(u, raw, c0, width):
+            cut = width * VECTOR_EIGHTHS // 8
             shares = ((nc.vector.tensor_copy, 0, cut), (nc.scalar.copy, cut, width))
-            for copy, a, b in shares if width > 256 else ((nc.vector.tensor_copy, 0, width),):
+            if width <= UNSHARED_WIDTH:
+                shares = ((nc.vector.tensor_copy, 0, width),)
+            for copy, lo, hi in shares:
                 copy(
-                    pairs[u][:, 2 * (c0 + a) : 2 * (c0 + b)].rearrange("p (c i e) -> p c e i", i=4, e=2),
-                    raw[:, :, a:b].rearrange("p e (c i) -> p c e i", i=4),
+                    pairs[u][:, 2 * (c0 + lo) : 2 * (c0 + hi)].rearrange("p (c i e) -> p c e i", i=RUN, e=2),
+                    raw[:, :, lo:hi].rearrange("p e (c i) -> p c e i", i=RUN),
                 )
 
-        def gather_pairs(u):
+        def gather_pair(u):
             window = pairs[u][:].bitcast(U32)
-            nc.vector.tensor_copy(picked[:, u, :], window.indirect(offs_t[:, 0 : HALF // 16]))
+            nc.vector.tensor_copy(picked[:, u, :], window.indirect(offs_t[:, 0 : HALF // PER_COLUMN]))
             nc.vector.tensor_copy(
-                x_bf1[:].bitcast(U32).rearrange("p (n u) -> p n u", u=2)[:, :, u],
-                window.indirect(offs_t[:, HALF // 16 : S // 16]),
+                x_second[:].bitcast(U32).rearrange("p (n u) -> p n u", u=2)[:, :, u],
+                window.indirect(offs_t[:, HALF // PER_COLUMN : S // PER_COLUMN]),
             )
 
-        raws0 = load_chunks(0)
+        loads0 = load_pair(0)
         offs_t = load_list(offs, "offs_t")
-        raws1 = load_chunks(1)
-        w1_raw = load_weight(w1, "w1")
-        w2_raw = load_weight(w2, "w2")
+        loads1 = load_pair(1)
+        w1_raw = load_weight(w1, "w1_raw")
+        w2_raw = load_weight(w2, "w2_raw")
         cen_t = load_list(cen, "cen_t")
         pos_t = [load_list(pos1, "pos1_t"), load_list(pos2, "pos2_t")]
-        w3_raw = load_weight(w3, "w3")
+        w3_raw = load_weight(w3, "w3_raw")
 
-        for u, raws in enumerate((raws0, raws1)):
-            for raw, c0, width in raws:
-                round_chunk(u, raw, c0, width)
-            gather_pairs(u)
+        for u, loads in enumerate((loads0, loads1)):
+            for raw, c0, width in loads:
+                round_load(u, raw, c0, width)
+            gather_pair(u)
 
-        w1_bf = round_weight(w1_raw, 0, N, "w1", "w1_bf")
-        x_bf0 = keep.tile([P, 4 * HALF], BF16, name="x_bf0", tag="w1_raw", align_bytes=256)
+        w1_bf = round_weight(w1_raw, "w1_bf", "w1_bf")
+        x_first = keep.tile([P, 4 * HALF], BF16, name="x_first", tag="w1_raw", align_bytes=ALIGN)
         nc.scalar.copy(
-            x_bf0[:].bitcast(U32).rearrange("p (n u) -> p n u", u=2),
+            x_first[:].bitcast(U32).rearrange("p (n u) -> p n u", u=2),
             picked[:].rearrange("p u n -> p n u"),
         )
-        w2_bf = round_weight(w2_raw, 0, N, "w2", "picked")
-        w1_q = quantize(w1_bf[:], N, "w1", "w1_codes")
-        x_q = [
-            quantize(x_bf1[:], HALF, "x1", "w1_bf"),
-            quantize(x_bf0[:], HALF, "x0", "x0_codes"),
-        ][::-1]
-        w2_q = quantize(w2_bf[:], N, "w2", "w2_codes")
+        w2_bf = round_weight(w2_raw, "w2_bf", "picked")
 
-        def product(w_q, b, name, bank, first_copy=nc.scalar.copy, order=(0, 1)):
-            rows = keep.tile([P, S], F32, name=name, tag="w1_raw" if name == "y0" else name, align_bytes=256)
-            cols = slice(b * P, (b + 1) * P)
-            for i, a in enumerate(order):
-                copy = first_copy if i == 0 else nc.scalar.copy
-                acc = psum.tile([P, HALF], F32, name="acc", tag="bank%d" % ((bank + i) % 3))
+        w1_q = quantize(w1_bf, N, "w1", "w1_codes")
+        x_second_q = quantize(x_second, HALF, "x_second", "w1_bf")
+        x_first_q = quantize(x_first, HALF, "x_first", "x_first_codes", parts=2)
+        x_q = [x_first_q, x_second_q]
+
+        def product(w_q, block, name, tag, pieces):
+            rows = keep.tile([P, S], F32, name=name, tag=tag, align_bytes=ALIGN)
+            cols = slice(block * P, (block + 1) * P)
+            for c0, c1, bank, copy in pieces:
+                half = c0 // HALF
+                nodes = slice(c0 - half * HALF, c1 - half * HALF)
+                acc = psum.tile([P, c1 - c0], F32, name="acc", tag="bank%d" % bank)
                 nc.tensor.matmul_mx(
                     out=acc[:],
                     lhsT=w_q[0][:, cols].bitcast(FP8X4),
                     lhsT_scale=w_q[1][:, cols],
-                    rhs=x_q[a][0][:].bitcast(FP8X4),
-                    rhs_scale=x_q[a][1][:],
+                    rhs=x_q[half][0][:, nodes].bitcast(FP8X4),
+                    rhs_scale=x_q[half][1][:, nodes],
                     start=True,
                     stop=True,
                 )
-                copy(rows[:, a * HALF : (a + 1) * HALF], acc[:])
+                copy(rows[:, c0:c1], acc[:])
             return rows
+
+        def halves(turn):
+            return [(half * HALF, (half + 1) * HALF, (2 * turn + half) % RING, nc.scalar.copy) for half in range(2)]
 
         def centres(y, name):
             yc = keep.tile([P, V], F32, name=name)
             nc.vector.tensor_copy(yc[:], y[:].indirect(cen_t[:]))
             return yc
 
-        def sums(b, yc, e):
-            res = []
+        def gate_inputs(block, yc, e):
+            sums = []
             for d in range(2):
-                pre = keep.tile([P, V], F32, name="pre%d_%d" % (b, d))
+                pre = keep.tile([P, V], F32, name="pre%d_%d" % (block, d))
                 nc.vector.tensor_tensor(pre[:], e[:].indirect(pos_t[d][:]), yc[:], ALU.add)
-                res.append(pre)
-            return res
+                sums.append(pre)
+            return sums
 
         def sigmoid(pre, name):
             gate = keep.tile([P, V], F32, name=name, tag=name)
@@ -152,47 +170,56 @@ def tile_picked_gatedg_relu_e_kernel(tc, xT, w1, w2, w3, offs, cen, pos1, pos2, 
         def message(h, gate, d, name, parts=1):
             msg = keep.tile([P, V], F32, name=name)
             width = V // parts
-            for i in range(parts):
-                cols = slice(i * width, (i + 1) * width)
-                entries = pos_t[d][:, i * width // 16 : (i + 1) * width // 16]
+            for c0 in range(0, V, width):
+                cols = slice(c0, c0 + width)
+                entries = pos_t[d][:, c0 // PER_COLUMN : (c0 + width) // PER_COLUMN]
                 nc.vector.tensor_tensor(msg[:, cols], h[:].indirect(entries), gate[:, cols], ALU.mult)
             return msg
 
-        def finish(b, msg, parts):
-            width = V // parts
+        def relu_on_scalar(res, total):
+            nc.scalar.activation(res, total, ACT.Relu)
+
+        def relu_on_vector(res, total):
+            nc.vector.tensor_scalar_max(res, total, 0.0)
+
+        def finish(block, msgs, tags, relu):
+            width = V // len(tags)
             totals = []
-            for i in range(parts):
+            for i, tag in enumerate(tags):
                 cols = slice(i * width, (i + 1) * width)
-                tag = "gate10" if b == 0 else "total%d" % i
-                total = keep.tile([P, width], F32, name="total%d_%d" % (b, i), tag=tag)
-                nc.vector.tensor_tensor(total[:], msg[0][:, cols], msg[1][:, cols], ALU.add)
+                total = keep.tile([P, width], F32, name="total%d_%d" % (block, i), tag=tag)
+                nc.vector.tensor_tensor(total[:], msgs[0][:, cols], msgs[1][:, cols], ALU.add)
                 totals.append(total)
             for i, total in enumerate(totals):
-                res = keep.tile([P, width], F32, name="res%d_%d" % (b, i))
-                if b == 1:
-                    nc.vector.tensor_scalar_max(res[:], total[:], 0.0)
-                else:
-                    nc.scalar.activation(res[:], total[:], ACT.Relu)
-                nc.sync.dma_start(out[b * P : (b + 1) * P, i * width : (i + 1) * width], res[:])
+                res = keep.tile([P, width], F32, name="res%d_%d" % (block, i))
+                relu(res[:], total[:])
+                nc.sync.dma_start(out[block * P : (block + 1) * P, i * width : (i + 1) * width], res[:])
 
-        y0 = product(w1_q, 0, "y0", 0, first_copy=nc.vector.tensor_copy, order=(1, 0))
+        y0_pieces = [
+            (HALF, S, 0, nc.vector.tensor_copy),
+            (0, HALF // 2, RING, nc.vector.tensor_copy),
+            (HALF // 2, HALF, 1, nc.scalar.copy),
+        ]
+        y0 = product(w1_q, 0, "y0", "w1_raw", y0_pieces)
+        w2_q = quantize(w2_bf, N, "w2", "w2_codes")
+
         yc0 = centres(y0, "yc0")
-        y1 = product(w1_q, 1, "y1", 2)
+        y1 = product(w1_q, 1, "y1", "y1", halves(1))
         yc1 = centres(y1, "yc1")
-        e0 = product(w2_q, 0, "e0", 4)
-        pre0 = sums(0, yc0, e0)
-        w3_q = quantize(round_weight(w3_raw, 0, N, "w3", "y1")[:], N, "w3", "w3_codes")
-        e1 = product(w2_q, 1, "e1", 6)
-        pre1 = sums(1, yc1, e1)
-        g00 = sigmoid(pre0[0], "gate00")
-        g01 = sigmoid(pre0[1], "gate01")
-        h0 = product(w3_q, 0, "h0", 8)
-        h1 = product(w3_q, 1, "h1", 10)
-        g10 = sigmoid(pre1[0], "gate10")
-        g11 = sigmoid(pre1[1], "gate11")
-        m00 = message(h0, g00, 0, "msg00")
-        m01 = message(h0, g01, 1, "msg01")
-        m10 = message(h1, g10, 0, "msg10")
-        finish(0, [m00, m01], 1)
-        m11 = message(h1, g11, 1, "msg11", 2)
-        finish(1, [m10, m11], 2)
+        e0 = product(w2_q, 0, "e0", "e0", halves(2))
+        pre0 = gate_inputs(0, yc0, e0)
+        w3_q = quantize(round_weight(w3_raw, "w3_bf", "y1"), N, "w3", "w3_codes")
+        e1 = product(w2_q, 1, "e1", "e1", halves(3))
+        pre1 = gate_inputs(1, yc1, e1)
+        gate00 = sigmoid(pre0[0], "gate00")
+        gate01 = sigmoid(pre0[1], "gate01")
+        h0 = product(w3_q, 0, "h0", "h0", halves(4))
+        h1 = product(w3_q, 1, "h1", "h1", halves(5))
+        gate10 = sigmoid(pre1[0], "gate10")
+        gate11 = sigmoid(pre1[1], "gate11")
+        msg00 = message(h0, gate00, 0, "msg00")
+        msg01 = message(h0, gate01, 1, "msg01")
+        msg10 = message(h1, gate10, 0, "msg10")
+        finish(0, [msg00, msg01], ["gate10"], relu_on_scalar)
+        msg11 = message(h1, gate11, 1, "msg11", parts=2)
+        finish(1, [msg10, msg11], ["total_a", "total_b"], relu_on_vector)

@@ -16,13 +16,13 @@ ALU = mybir.AluOpType
 
 P = 128
 HALF = S // 2
+QUARTER = S // 4
 PER_COLUMN = 16
 RUN = 4
 ALIGN = 256
 
-LOADS = ((2048, 2048), (2048, 1024, 512, 256, 256))
-VECTOR_EIGHTHS = 5
-UNSHARED_WIDTH = 256
+LOADS = ((4096,), (4096,), (2048, 2048), (2048, 1024, 512, 384, 128))
+VECTOR_QUARTERS = 3
 RING = 3
 
 
@@ -42,14 +42,14 @@ def tile_picked_gatedg_relu_e_kernel(tc, xT, w1, w2, w3, offs, cen, pos1, pos2, 
             nc.sync.dma_start(entries[:], src)
             return entries
 
-        def load_weight(w, name):
-            raw = keep.tile([P, 4, N], F32, name=name, tag=name, align_bytes=ALIGN)
-            nc.sync.dma_start(raw[:], w.rearrange("(p j) n -> p j n", j=4))
+        def load_weight(w, c0, c1, name):
+            raw = keep.tile([P, 4, c1 - c0], F32, name=name, tag=name, align_bytes=ALIGN)
+            nc.sync.dma_start(raw[:], w.rearrange("(p j) n -> p j n", j=4)[:, :, c0:c1])
             return raw
 
-        def round_weight(raw, name, tag):
-            grouped = keep.tile([P, N * 4], BF16, name=name, tag=tag, align_bytes=ALIGN)
-            nc.scalar.copy(
+        def round_weight(copy, raw, name, tag):
+            grouped = keep.tile([P, raw.shape[2] * 4], BF16, name=name, tag=tag, align_bytes=ALIGN)
+            copy(
                 grouped[:].rearrange("p (c i j) -> p c j i", i=RUN, j=4),
                 raw[:].rearrange("p j (c i) -> p c j i", i=RUN),
             )
@@ -67,77 +67,75 @@ def tile_picked_gatedg_relu_e_kernel(tc, xT, w1, w2, w3, offs, cen, pos1, pos2, 
                 )
             return codes, scales
 
-        x_rows = xT.rearrange("(p u e) t -> p u e t", u=2, e=2)
-        pairs = [keep.tile([P, 2 * T], BF16, name="pairs%d" % u) for u in range(2)]
-        picked = keep.tile([P, 2, HALF], U32, name="picked", tag="picked", align_bytes=ALIGN)
-        x_second = keep.tile([P, 4 * HALF], BF16, name="x_second", align_bytes=ALIGN)
+        x_rows = xT.rearrange("(p j) t -> p j t", j=4)
+        planes = [keep.tile([P, T], F32, name="plane%d" % j, align_bytes=ALIGN) for j in range(4)]
+        rounded = [keep.tile([P, T], BF16, name="rounded%d" % j, align_bytes=ALIGN) for j in range(4)]
+        x_first = keep.tile([P, 4 * HALF], BF16, name="x_first", tag="x_first", align_bytes=ALIGN)
+        x_second = keep.tile([P, 4 * HALF], BF16, name="x_second", tag="x_second", align_bytes=ALIGN)
 
-        def load_pair(u):
-            loads, c0 = [], 0
-            for width in LOADS[u]:
-                raw = keep.tile([P, 2, width], F32, name="x_raw%d_%d" % (u, c0), align_bytes=ALIGN)
-                nc.sync.dma_start(raw[:], x_rows[:, u, :, c0 : c0 + width])
-                loads.append((raw, c0, width))
+        def load_plane(j):
+            c0 = 0
+            for width in LOADS[j]:
+                nc.sync.dma_start(planes[j][:, c0 : c0 + width], x_rows[:, j, c0 : c0 + width])
                 c0 = c0 + width
-            return loads
 
-        def round_load(u, raw, c0, width):
-            cut = width * VECTOR_EIGHTHS // 8
-            shares = ((nc.vector.tensor_copy, 0, cut), (nc.scalar.copy, cut, width))
-            if width <= UNSHARED_WIDTH:
-                shares = ((nc.vector.tensor_copy, 0, width),)
-            for copy, lo, hi in shares:
-                copy(
-                    pairs[u][:, 2 * (c0 + lo) : 2 * (c0 + hi)].rearrange("p (c i e) -> p c e i", i=RUN, e=2),
-                    raw[:, :, lo:hi].rearrange("p e (c i) -> p c e i", i=RUN),
-                )
+        def round_plane(j):
+            c0 = 0
+            for width in LOADS[j]:
+                cut = c0 + width * VECTOR_QUARTERS // 4
+                if c0 + width == T and j == 3:
+                    cut = c0
+                if cut > c0:
+                    nc.vector.tensor_copy(rounded[j][:, c0:cut], planes[j][:, c0:cut])
+                nc.scalar.copy(rounded[j][:, cut : c0 + width], planes[j][:, cut : c0 + width])
+                c0 = c0 + width
 
-        def gather_pair(u):
-            window = pairs[u][:].bitcast(U32)
-            nc.vector.tensor_copy(picked[:, u, :], window.indirect(offs_t[:, 0 : HALF // PER_COLUMN]))
+        def gather_plane(j):
             nc.vector.tensor_copy(
-                x_second[:].bitcast(U32).rearrange("p (n u) -> p n u", u=2)[:, :, u],
-                window.indirect(offs_t[:, HALF // PER_COLUMN : S // PER_COLUMN]),
+                x_first[:].rearrange("p (n j) -> p n j", j=4)[:, :, j],
+                planes[j][:].indirect(offs_t[:, 0 : HALF // PER_COLUMN]),
+            )
+            nc.scalar.activation(
+                x_second[:].rearrange("p (n j) -> p n j", j=4)[:, :, j],
+                rounded[j][:].indirect(offs_t[:, HALF // PER_COLUMN : S // PER_COLUMN]),
+                ACT.Copy,
             )
 
-        loads0 = load_pair(0)
+        load_plane(0)
         offs_t = load_list(offs, "offs_t")
-        loads1 = load_pair(1)
-        w1_raw = load_weight(w1, "w1_raw")
-        w2_raw = load_weight(w2, "w2_raw")
+        for j in range(1, 4):
+            load_plane(j)
+        w10_raw = load_weight(w1, 0, P, "w10_raw")
+        w20_raw = load_weight(w2, 0, P, "w20_raw")
+        w11_raw = load_weight(w1, P, N, "w11_raw")
+        w21_raw = load_weight(w2, P, N, "w21_raw")
         cen_t = load_list(cen, "cen_t")
         pos_t = [load_list(pos1, "pos1_t"), load_list(pos2, "pos2_t")]
-        w3_raw = load_weight(w3, "w3_raw")
+        w3_raw = load_weight(w3, 0, N, "w3_raw")
 
-        for u, loads in enumerate((loads0, loads1)):
-            for raw, c0, width in loads:
-                round_load(u, raw, c0, width)
-            gather_pair(u)
+        for j in range(4):
+            round_plane(j)
+            gather_plane(j)
 
-        w1_bf = round_weight(w1_raw, "w1_bf", "w1_bf")
-        x_first = keep.tile([P, 4 * HALF], BF16, name="x_first", tag="w1_raw", align_bytes=ALIGN)
-        nc.scalar.copy(
-            x_first[:].bitcast(U32).rearrange("p (n u) -> p n u", u=2),
-            picked[:].rearrange("p u n -> p n u"),
-        )
-        w2_bf = round_weight(w2_raw, "w2_bf", "picked")
-
-        w1_q = quantize(w1_bf, N, "w1", "w1_codes")
-        x_second_q = quantize(x_second, HALF, "x_second", "w1_bf")
-        x_first_q = quantize(x_first, HALF, "x_first", "x_first_codes", parts=2)
+        w10_bf = round_weight(nc.vector.tensor_copy, w10_raw, "w10_bf", "w10_bf")
+        w20_bf = round_weight(nc.scalar.copy, w20_raw, "w20_bf", "w20_bf")
+        w10_q = quantize(w10_bf, P, "w10", "w10_codes")
+        x_first_q = quantize(x_first, HALF, "x_first", "w10_raw")
+        x_second_q = quantize(x_second, HALF, "x_second", "x_second_codes", parts=2)
         x_q = [x_first_q, x_second_q]
+        w20_q = quantize(w20_bf, P, "w20", "w20_codes")
+        w11_bf = round_weight(nc.vector.tensor_copy, w11_raw, "w11_bf", "w11_bf")
 
-        def product(w_q, block, name, tag, pieces):
+        def product(w_q, w0, name, tag, pieces):
             rows = keep.tile([P, S], F32, name=name, tag=tag, align_bytes=ALIGN)
-            cols = slice(block * P, (block + 1) * P)
             for c0, c1, bank, copy in pieces:
                 half = c0 // HALF
                 nodes = slice(c0 - half * HALF, c1 - half * HALF)
                 acc = psum.tile([P, c1 - c0], F32, name="acc", tag="bank%d" % bank)
                 nc.tensor.matmul_mx(
                     out=acc[:],
-                    lhsT=w_q[0][:, cols].bitcast(FP8X4),
-                    lhsT_scale=w_q[1][:, cols],
+                    lhsT=w_q[0][:, w0 : w0 + P].bitcast(FP8X4),
+                    lhsT_scale=w_q[1][:, w0 : w0 + P],
                     rhs=x_q[half][0][:, nodes].bitcast(FP8X4),
                     rhs_scale=x_q[half][1][:, nodes],
                     start=True,
@@ -149,31 +147,35 @@ def tile_picked_gatedg_relu_e_kernel(tc, xT, w1, w2, w3, offs, cen, pos1, pos2, 
         def halves(turn):
             return [(half * HALF, (half + 1) * HALF, (2 * turn + half) % RING, nc.scalar.copy) for half in range(2)]
 
-        def centres(y, name):
-            yc = keep.tile([P, V], F32, name=name)
-            nc.vector.tensor_copy(yc[:], y[:].indirect(cen_t[:]))
+        def entries(lst, c0, c1):
+            return lst[:, c0 // PER_COLUMN : c1 // PER_COLUMN]
+
+        def centres(y, name, parts=1):
+            yc = keep.tile([P, V], F32, name=name, align_bytes=ALIGN)
+            width = V // parts
+            for c0 in range(0, V, width):
+                nc.vector.tensor_copy(yc[:, c0 : c0 + width], y[:].indirect(entries(cen_t, c0, c0 + width)))
             return yc
 
-        def gate_inputs(block, yc, e):
-            sums = []
-            for d in range(2):
-                pre = keep.tile([P, V], F32, name="pre%d_%d" % (block, d))
-                nc.vector.tensor_tensor(pre[:], e[:].indirect(pos_t[d][:]), yc[:], ALU.add)
-                sums.append(pre)
-            return sums
-
-        def sigmoid(pre, name):
-            gate = keep.tile([P, V], F32, name=name, tag=name)
-            nc.scalar.activation(gate[:], pre[:], ACT.Sigmoid)
-            return gate
-
-        def message(h, gate, d, name, parts=1):
-            msg = keep.tile([P, V], F32, name=name)
+        def gate_input(yc, e, d, name, tag, parts=1):
+            pre = keep.tile([P, V], F32, name=name, tag=tag, align_bytes=ALIGN)
             width = V // parts
             for c0 in range(0, V, width):
                 cols = slice(c0, c0 + width)
-                entries = pos_t[d][:, c0 // PER_COLUMN : (c0 + width) // PER_COLUMN]
-                nc.vector.tensor_tensor(msg[:, cols], h[:].indirect(entries), gate[:, cols], ALU.mult)
+                nc.vector.tensor_tensor(pre[:, cols], e[:].indirect(entries(pos_t[d], c0, c0 + width)), yc[:, cols], ALU.add)
+            return pre
+
+        def sigmoid(pre, name):
+            gate = keep.tile([P, V], F32, name=name, tag=name, align_bytes=ALIGN)
+            nc.scalar.activation(gate[:], pre[:], ACT.Sigmoid)
+            return gate
+
+        def message(h, gate, d, name, tag, parts=1):
+            msg = keep.tile([P, V], F32, name=name, tag=tag, align_bytes=ALIGN)
+            width = V // parts
+            for c0 in range(0, V, width):
+                cols = slice(c0, c0 + width)
+                nc.vector.tensor_tensor(msg[:, cols], h[:].indirect(entries(pos_t[d], c0, c0 + width)), gate[:, cols], ALU.mult)
             return msg
 
         def relu_on_scalar(res, total):
@@ -187,7 +189,7 @@ def tile_picked_gatedg_relu_e_kernel(tc, xT, w1, w2, w3, offs, cen, pos1, pos2, 
             totals = []
             for i, tag in enumerate(tags):
                 cols = slice(i * width, (i + 1) * width)
-                total = keep.tile([P, width], F32, name="total%d_%d" % (block, i), tag=tag)
+                total = keep.tile([P, width], F32, name="total%d_%d" % (block, i), tag=tag, align_bytes=ALIGN)
                 nc.vector.tensor_tensor(total[:], msgs[0][:, cols], msgs[1][:, cols], ALU.add)
                 totals.append(total)
             for i, total in enumerate(totals):
@@ -196,30 +198,32 @@ def tile_picked_gatedg_relu_e_kernel(tc, xT, w1, w2, w3, offs, cen, pos1, pos2, 
                 nc.sync.dma_start(out[block * P : (block + 1) * P, i * width : (i + 1) * width], res[:])
 
         y0_pieces = [
-            (HALF, S, 0, nc.vector.tensor_copy),
-            (0, HALF // 2, RING, nc.vector.tensor_copy),
-            (HALF // 2, HALF, 1, nc.scalar.copy),
+            (0, HALF, RING, nc.scalar.copy),
+            (HALF, HALF + QUARTER, RING + 1, nc.scalar.copy),
+            (HALF + QUARTER, S, RING + 2, nc.vector.tensor_copy),
         ]
-        y0 = product(w1_q, 0, "y0", "w1_raw", y0_pieces)
-        w2_q = quantize(w2_bf, N, "w2", "w2_codes")
-
-        yc0 = centres(y0, "yc0")
-        y1 = product(w1_q, 1, "y1", "y1", halves(1))
+        y0 = product(w10_q, 0, "y0", "y0", y0_pieces)
+        w11_q = quantize(w11_bf, P, "w11", "w10_codes")
+        yc0 = centres(y0, "yc0", parts=2)
+        e0 = product(w20_q, 0, "e0", "e0", halves(0))
+        pre00 = gate_input(yc0, e0, 0, "pre00", "pre00", parts=2)
+        w21_q = quantize(round_weight(nc.scalar.copy, w21_raw, "w21_bf", "w20_codes"), P, "w21", "w21_codes")
+        pre01 = gate_input(yc0, e0, 1, "pre01", "w21_raw")
+        y1 = product(w11_q, 0, "y1", "y1", halves(1))
         yc1 = centres(y1, "yc1")
-        e0 = product(w2_q, 0, "e0", "e0", halves(2))
-        pre0 = gate_inputs(0, yc0, e0)
-        w3_q = quantize(round_weight(w3_raw, "w3_bf", "y1"), N, "w3", "w3_codes")
-        e1 = product(w2_q, 1, "e1", "e1", halves(3))
-        pre1 = gate_inputs(1, yc1, e1)
-        gate00 = sigmoid(pre0[0], "gate00")
-        gate01 = sigmoid(pre0[1], "gate01")
-        h0 = product(w3_q, 0, "h0", "h0", halves(4))
-        h1 = product(w3_q, 1, "h1", "h1", halves(5))
-        gate10 = sigmoid(pre1[0], "gate10")
-        gate11 = sigmoid(pre1[1], "gate11")
-        msg00 = message(h0, gate00, 0, "msg00")
-        msg01 = message(h0, gate01, 1, "msg01")
-        msg10 = message(h1, gate10, 0, "msg10")
-        finish(0, [msg00, msg01], ["gate10"], relu_on_scalar)
-        msg11 = message(h1, gate11, 1, "msg11", parts=2)
+        w3_q = quantize(round_weight(nc.scalar.copy, w3_raw, "w3_bf", "w10_codes"), N, "w3", "w3_codes")
+        e1 = product(w21_q, 0, "e1", "e1", halves(2))
+        pre10 = gate_input(yc1, e1, 0, "pre10", "pre10")
+        pre11 = gate_input(yc1, e1, 1, "pre11", "pre11")
+        gate00 = sigmoid(pre00, "gate00")
+        gate01 = sigmoid(pre01, "gate01")
+        h0 = product(w3_q, 0, "h0", "h0", halves(3))
+        gate10 = sigmoid(pre10, "gate10")
+        h1 = product(w3_q, P, "h1", "h1", halves(4))
+        gate11 = sigmoid(pre11, "gate11")
+        msg00 = message(h0, gate00, 0, "msg00", "msg00")
+        msg01 = message(h0, gate01, 1, "msg01", "msg01")
+        msg10 = message(h1, gate10, 0, "msg10", "msg10")
+        finish(0, [msg00, msg01], ["pre11"], relu_on_scalar)
+        msg11 = message(h1, gate11, 1, "msg11", "msg11", parts=2)
         finish(1, [msg10, msg11], ["total_a", "total_b"], relu_on_vector)

@@ -1,6 +1,7 @@
 from contextlib import ExitStack
 
 import concourse.mybir as mybir
+from concourse.masks import make_identity
 
 K, T, S, V, N = 512, 4096, 1024, 512, 256
 FLOPS = 3 * 2 * K * N * S
@@ -36,6 +37,9 @@ def tile_picked_gatedg_relu_e_kernel(tc, xT, w1, w2, w3, offs, cen, pos1, pos2, 
         warm_out = keep.tile([P, 8], F32, name="warm_out")
         nc.vector.memset(warm_in[:], 0.0)
         nc.scalar.activation(warm_out[:], warm_in[:], ACT.Sigmoid)
+
+        identity = keep.tile([P, P], F32, name="identity", align_bytes=ALIGN)
+        make_identity(nc, identity[:])
 
         def load_list(src, name):
             entries = keep.tile(list(src.shape), U16, name=name)
@@ -120,7 +124,7 @@ def tile_picked_gatedg_relu_e_kernel(tc, xT, w1, w2, w3, offs, cen, pos1, pos2, 
         w10_bf = round_weight(nc.vector.tensor_copy, w10_raw, "w10_bf", "w10_bf")
         w20_bf = round_weight(nc.scalar.copy, w20_raw, "w20_bf", "w20_bf")
         w10_q = quantize(w10_bf, P, "w10", "w10_codes")
-        x_first_q = quantize(x_first, HALF, "x_first", "w10_raw")
+        x_first_q = quantize(x_first, HALF, "x_first", "w10_raw", parts=2)
         x_second_q = quantize(x_second, HALF, "x_second", "x_second_codes", parts=2)
         x_q = [x_first_q, x_second_q]
         w20_q = quantize(w20_bf, P, "w20", "w20_codes")
@@ -128,24 +132,26 @@ def tile_picked_gatedg_relu_e_kernel(tc, xT, w1, w2, w3, offs, cen, pos1, pos2, 
 
         def product(w_q, w0, name, tag, pieces):
             rows = keep.tile([P, S], F32, name=name, tag=tag, align_bytes=ALIGN)
-            for c0, c1, bank, copy in pieces:
+            for c0, c1, bank, copy, parts in pieces:
                 half = c0 // HALF
-                nodes = slice(c0 - half * HALF, c1 - half * HALF)
                 acc = psum.tile([P, c1 - c0], F32, name="acc", tag="bank%d" % bank)
-                nc.tensor.matmul_mx(
-                    out=acc[:],
-                    lhsT=w_q[0][:, w0 : w0 + P].bitcast(FP8X4),
-                    lhsT_scale=w_q[1][:, w0 : w0 + P],
-                    rhs=x_q[half][0][:, nodes].bitcast(FP8X4),
-                    rhs_scale=x_q[half][1][:, nodes],
-                    start=True,
-                    stop=True,
-                )
+                width = (c1 - c0) // parts
+                for lo in range(0, c1 - c0, width):
+                    nodes = slice(c0 - half * HALF + lo, c0 - half * HALF + lo + width)
+                    nc.tensor.matmul_mx(
+                        out=acc[:, lo : lo + width],
+                        lhsT=w_q[0][:, w0 : w0 + P].bitcast(FP8X4),
+                        lhsT_scale=w_q[1][:, w0 : w0 + P],
+                        rhs=x_q[half][0][:, nodes].bitcast(FP8X4),
+                        rhs_scale=x_q[half][1][:, nodes],
+                        start=True,
+                        stop=True,
+                    )
                 copy(rows[:, c0:c1], acc[:])
             return rows
 
         def halves(turn):
-            return [(half * HALF, (half + 1) * HALF, (2 * turn + half) % RING, nc.scalar.copy) for half in range(2)]
+            return [(half * HALF, (half + 1) * HALF, (2 * turn + half) % RING, nc.scalar.copy, 1) for half in range(2)]
 
         def entries(lst, c0, c1):
             return lst[:, c0 // PER_COLUMN : c1 // PER_COLUMN]
@@ -178,8 +184,27 @@ def tile_picked_gatedg_relu_e_kernel(tc, xT, w1, w2, w3, offs, cen, pos1, pos2, 
                 nc.vector.tensor_tensor(msg[:, cols], h[:].indirect(entries(pos_t[d], c0, c0 + width)), gate[:, cols], ALU.mult)
             return msg
 
-        def relu_on_scalar(res, total):
-            nc.scalar.activation(res, total, ACT.Relu)
+        def finish_on_tensor(block, msgs, parts):
+            width = V // parts
+            turned_relu = []
+            for i in range(parts):
+                turned = psum.tile([P, width], F32, name="turned", tag="bank%d" % (RING + i))
+                steps = [(msg, c0) for msg in msgs for c0 in range(0, width, P)]
+                for n, (msg, c0) in enumerate(steps):
+                    nc.tensor.matmul(
+                        turned[:, c0 : c0 + P], lhsT=msg[:, i * width + c0 : i * width + c0 + P], rhs=identity[:],
+                        is_transpose=True, start=(n == 0), stop=(n == len(steps) - 1),
+                    )
+                part = keep.tile([P, width], F32, name="turned_relu%d" % i, align_bytes=ALIGN)
+                nc.scalar.activation(part[:], turned[:], ACT.Relu)
+                turned_relu.append(part)
+            for i, part in enumerate(turned_relu):
+                back = psum.tile([P, width], F32, name="back", tag="back%d" % i)
+                for c0 in range(0, width, P):
+                    nc.tensor.transpose(back[:, c0 : c0 + P], part[:, c0 : c0 + P], identity[:])
+                res = keep.tile([P, width], F32, name="res%d_%d" % (block, i))
+                nc.scalar.copy(res[:], back[:])
+                nc.sync.dma_start(out[block * P : (block + 1) * P, i * width : (i + 1) * width], res[:])
 
         def relu_on_vector(res, total):
             nc.vector.tensor_scalar_max(res, total, 0.0)
@@ -198,9 +223,9 @@ def tile_picked_gatedg_relu_e_kernel(tc, xT, w1, w2, w3, offs, cen, pos1, pos2, 
                 nc.sync.dma_start(out[block * P : (block + 1) * P, i * width : (i + 1) * width], res[:])
 
         y0_pieces = [
-            (0, HALF, RING, nc.scalar.copy),
-            (HALF, HALF + QUARTER, RING + 1, nc.scalar.copy),
-            (HALF + QUARTER, S, RING + 2, nc.vector.tensor_copy),
+            (0, HALF, RING, nc.scalar.copy, 2),
+            (HALF, HALF + QUARTER, RING + 1, nc.scalar.copy, 1),
+            (HALF + QUARTER, S, RING + 2, nc.vector.tensor_copy, 1),
         ]
         y0 = product(w10_q, 0, "y0", "y0", y0_pieces)
         w11_q = quantize(w11_bf, P, "w11", "w10_codes")
@@ -224,6 +249,6 @@ def tile_picked_gatedg_relu_e_kernel(tc, xT, w1, w2, w3, offs, cen, pos1, pos2, 
         msg00 = message(h0, gate00, 0, "msg00", "msg00")
         msg01 = message(h0, gate01, 1, "msg01", "msg01")
         msg10 = message(h1, gate10, 0, "msg10", "msg10")
-        finish(0, [msg00, msg01], ["pre11"], relu_on_scalar)
+        finish_on_tensor(0, [msg00, msg01], 2)
         msg11 = message(h1, gate11, 1, "msg11", "msg11", parts=2)
         finish(1, [msg10, msg11], ["total_a", "total_b"], relu_on_vector)

@@ -22,8 +22,9 @@ PER_COLUMN = 16
 RUN = 4
 ALIGN = 256
 
-LOADS = ((4096,), (4096,), (2048, 2048), (2048, 1024, 512, 384, 128))
-VECTOR_QUARTERS = 3
+LOADS = ((4096,), (4096,), (2048, 2048), (2048, 1536, 512))
+SHARED = (2, 3)
+VECTOR_THIRDS = 2
 RING = 3
 
 
@@ -51,29 +52,37 @@ def tile_picked_gatedg_relu_e_kernel(tc, xT, w1, w2, w3, offs, cen, pos1, pos2, 
             nc.sync.dma_start(raw[:], w.rearrange("(p j) n -> p j n", j=4)[:, :, c0:c1])
             return raw
 
-        def round_weight(copy, raw, name, tag):
-            grouped = keep.tile([P, raw.shape[2] * 4], BF16, name=name, tag=tag, align_bytes=ALIGN)
+        def round_weight(copy, raw, name, tag, c0=0):
+            grouped = keep.tile([P, P * 4], BF16, name=name, tag=tag, align_bytes=ALIGN)
             copy(
                 grouped[:].rearrange("p (c i j) -> p c j i", i=RUN, j=4),
-                raw[:].rearrange("p j (c i) -> p c j i", i=RUN),
+                raw[:, :, c0 : c0 + P].rearrange("p j (c i) -> p c j i", i=RUN),
             )
             return grouped
 
-        def quantize(grouped, width, name, tag, parts=1):
+        def code_tiles(width, name, tag):
             codes = keep.tile([P, width], U32, name=name + "_codes", tag=tag, align_bytes=ALIGN)
-            scales = keep.tile([P, width], U8, name=name + "_scales", align_bytes=64)
-            step = width // parts
-            for c0 in range(0, width, step):
-                nc.vector.quantize_mx(
-                    out=codes[:, c0 : c0 + step].bitcast(FP8X4),
-                    scales=scales[:, c0 : c0 + step],
-                    in_=grouped[:, 4 * c0 : 4 * (c0 + step)],
-                )
+            scales = keep.tile([P, width], U8, name=name + "_scales", tag=name + "_scales", align_bytes=ALIGN)
             return codes, scales
+
+        def quantize_columns(quantized, grouped, c0, c1):
+            nc.vector.quantize_mx(
+                out=quantized[0][:, c0:c1].bitcast(FP8X4),
+                scales=quantized[1][:, c0:c1],
+                in_=grouped[:, 4 * c0 : 4 * c1],
+            )
+
+        def quantize(grouped, widths, name, tag):
+            quantized = code_tiles(sum(widths), name, tag)
+            c0 = 0
+            for width in widths:
+                quantize_columns(quantized, grouped, c0, c0 + width)
+                c0 = c0 + width
+            return quantized
 
         x_rows = xT.rearrange("(p j) t -> p j t", j=4)
         planes = [keep.tile([P, T], F32, name="plane%d" % j, align_bytes=ALIGN) for j in range(4)]
-        rounded = [keep.tile([P, T], BF16, name="rounded%d" % j, align_bytes=ALIGN) for j in range(4)]
+        rounded = {j: keep.tile([P, T], BF16, name="rounded%d" % j, align_bytes=ALIGN) for j in SHARED}
         x_first = keep.tile([P, 4 * HALF], BF16, name="x_first", tag="x_first", align_bytes=ALIGN)
         x_second = keep.tile([P, 4 * HALF], BF16, name="x_second", tag="x_second", align_bytes=ALIGN)
 
@@ -86,9 +95,9 @@ def tile_picked_gatedg_relu_e_kernel(tc, xT, w1, w2, w3, offs, cen, pos1, pos2, 
         def round_plane(j):
             c0 = 0
             for width in LOADS[j]:
-                cut = c0 + width * VECTOR_QUARTERS // 4
+                cut = c0 + width * VECTOR_THIRDS // 3 // 16 * 16
                 if c0 + width == T and j == 3:
-                    cut = c0
+                    cut = c0 + width // 2
                 if cut > c0:
                     nc.vector.tensor_copy(rounded[j][:, c0:cut], planes[j][:, c0:cut])
                 nc.scalar.copy(rounded[j][:, cut : c0 + width], planes[j][:, cut : c0 + width])
@@ -99,11 +108,12 @@ def tile_picked_gatedg_relu_e_kernel(tc, xT, w1, w2, w3, offs, cen, pos1, pos2, 
                 x_first[:].rearrange("p (n j) -> p n j", j=4)[:, :, j],
                 planes[j][:].indirect(offs_t[:, 0 : HALF // PER_COLUMN]),
             )
-            nc.scalar.activation(
-                x_second[:].rearrange("p (n j) -> p n j", j=4)[:, :, j],
-                rounded[j][:].indirect(offs_t[:, HALF // PER_COLUMN : S // PER_COLUMN]),
-                ACT.Copy,
-            )
+            second = x_second[:].rearrange("p (n j) -> p n j", j=4)[:, :, j]
+            second_entries = offs_t[:, HALF // PER_COLUMN : S // PER_COLUMN]
+            if j in SHARED:
+                nc.scalar.activation(second, rounded[j][:].indirect(second_entries), ACT.Copy)
+            else:
+                nc.vector.tensor_copy(second, planes[j][:].indirect(second_entries))
 
         load_plane(0)
         offs_t = load_list(offs, "offs_t")
@@ -112,25 +122,28 @@ def tile_picked_gatedg_relu_e_kernel(tc, xT, w1, w2, w3, offs, cen, pos1, pos2, 
         w10_raw = load_weight(w1, 0, P, "w10_raw")
         w20_raw = load_weight(w2, 0, P, "w20_raw")
         w11_raw = load_weight(w1, P, N, "w11_raw")
-        w21_raw = load_weight(w2, P, N, "w21_raw")
         cen_t = load_list(cen, "cen_t")
+        w21_raw = load_weight(w2, P, N, "w21_raw")
         pos_t = [load_list(pos1, "pos1_t"), load_list(pos2, "pos2_t")]
         w3_raw = load_weight(w3, 0, N, "w3_raw")
 
         for j in range(4):
-            round_plane(j)
+            if j in SHARED:
+                round_plane(j)
             gather_plane(j)
 
         w10_bf = round_weight(nc.vector.tensor_copy, w10_raw, "w10_bf", "w10_bf")
         w20_bf = round_weight(nc.scalar.copy, w20_raw, "w20_bf", "w20_bf")
-        w10_q = quantize(w10_bf, P, "w10", "w10_codes")
-        x_first_q = quantize(x_first, HALF, "x_first", "w10_raw", parts=2)
-        x_second_q = quantize(x_second, HALF, "x_second", "x_second_codes", parts=2)
+        x_first_q = code_tiles(HALF, "x_first", "x_first_codes")
+        quantize_columns(x_first_q, x_first, 0, QUARTER)
+        w10_q = quantize(w10_bf, (P,), "w10", "w10_codes")
+        quantize_columns(x_first_q, x_first, QUARTER, HALF)
+        x_second_q = quantize(x_second, (QUARTER, P, P), "x_second", "x_second_codes")
         x_q = [x_first_q, x_second_q]
-        w20_q = quantize(w20_bf, P, "w20", "w20_codes")
+        w20_q = quantize(w20_bf, (P,), "w20", "w20_codes")
         w11_bf = round_weight(nc.vector.tensor_copy, w11_raw, "w11_bf", "w11_bf")
 
-        def product(w_q, w0, name, tag, pieces):
+        def product(w_q, name, tag, pieces):
             rows = keep.tile([P, S], F32, name=name, tag=tag, align_bytes=ALIGN)
             for c0, c1, bank, copy, parts in pieces:
                 half = c0 // HALF
@@ -140,8 +153,8 @@ def tile_picked_gatedg_relu_e_kernel(tc, xT, w1, w2, w3, offs, cen, pos1, pos2, 
                     nodes = slice(c0 - half * HALF + lo, c0 - half * HALF + lo + width)
                     nc.tensor.matmul_mx(
                         out=acc[:, lo : lo + width],
-                        lhsT=w_q[0][:, w0 : w0 + P].bitcast(FP8X4),
-                        lhsT_scale=w_q[1][:, w0 : w0 + P],
+                        lhsT=w_q[0][:].bitcast(FP8X4),
+                        lhsT_scale=w_q[1][:],
                         rhs=x_q[half][0][:, nodes].bitcast(FP8X4),
                         rhs_scale=x_q[half][1][:, nodes],
                         start=True,
@@ -199,7 +212,7 @@ def tile_picked_gatedg_relu_e_kernel(tc, xT, w1, w2, w3, offs, cen, pos1, pos2, 
                 nc.scalar.activation(part[:], turned[:], ACT.Relu)
                 turned_relu.append(part)
             for i, part in enumerate(turned_relu):
-                back = psum.tile([P, width], F32, name="back", tag="back%d" % i)
+                back = psum.tile([P, width], F32, name="back", tag="bank%d" % (RING + parts + i))
                 for c0 in range(0, width, P):
                     nc.tensor.transpose(back[:, c0 : c0 + P], part[:, c0 : c0 + P], identity[:])
                 res = keep.tile([P, width], F32, name="res%d_%d" % (block, i))
@@ -225,26 +238,28 @@ def tile_picked_gatedg_relu_e_kernel(tc, xT, w1, w2, w3, offs, cen, pos1, pos2, 
         y0_pieces = [
             (0, HALF, RING, nc.scalar.copy, 2),
             (HALF, HALF + QUARTER, RING + 1, nc.scalar.copy, 1),
-            (HALF + QUARTER, S, RING + 2, nc.vector.tensor_copy, 1),
+            (HALF + QUARTER, S - P, RING + 2, nc.scalar.copy, 1),
+            (S - P, S, RING + 3, nc.vector.tensor_copy, 1),
         ]
-        y0 = product(w10_q, 0, "y0", "y0", y0_pieces)
-        w11_q = quantize(w11_bf, P, "w11", "w10_codes")
+        y0 = product(w10_q, "y0", "y0", y0_pieces)
+        w11_q = quantize(w11_bf, (P,), "w11", "w10_codes")
         yc0 = centres(y0, "yc0", parts=2)
-        e0 = product(w20_q, 0, "e0", "e0", halves(0))
+        e0 = product(w20_q, "e0", "e0", halves(0))
         pre00 = gate_input(yc0, e0, 0, "pre00", "pre00", parts=2)
-        w21_q = quantize(round_weight(nc.scalar.copy, w21_raw, "w21_bf", "w20_codes"), P, "w21", "w21_codes")
+        w21_q = quantize(round_weight(nc.scalar.copy, w21_raw, "w21_bf", "w20_codes"), (P,), "w21", "w21_codes")
         pre01 = gate_input(yc0, e0, 1, "pre01", "w21_raw")
-        y1 = product(w11_q, 0, "y1", "y1", halves(1))
+        y1 = product(w11_q, "y1", "y1", halves(1))
         yc1 = centres(y1, "yc1")
-        w3_q = quantize(round_weight(nc.scalar.copy, w3_raw, "w3_bf", "w10_codes"), N, "w3", "w3_codes")
-        e1 = product(w21_q, 0, "e1", "e1", halves(2))
+        w30_q = quantize(round_weight(nc.scalar.copy, w3_raw, "w30_bf", "w10_codes"), (P,), "w30", "w30_codes")
+        e1 = product(w21_q, "e1", "e1", halves(2))
         pre10 = gate_input(yc1, e1, 0, "pre10", "pre10")
-        pre11 = gate_input(yc1, e1, 1, "pre11", "pre11")
         gate00 = sigmoid(pre00, "gate00")
+        w31_q = quantize(round_weight(nc.scalar.copy, w3_raw, "w31_bf", "w21_codes", P), (P,), "w31", "w31_codes")
+        pre11 = gate_input(yc1, e1, 1, "pre11", "w3_raw")
+        h0 = product(w30_q, "h0", "h0", halves(3))
         gate01 = sigmoid(pre01, "gate01")
-        h0 = product(w3_q, 0, "h0", "h0", halves(3))
+        h1 = product(w31_q, "h1", "h1", halves(4))
         gate10 = sigmoid(pre10, "gate10")
-        h1 = product(w3_q, P, "h1", "h1", halves(4))
         gate11 = sigmoid(pre11, "gate11")
         msg00 = message(h0, gate00, 0, "msg00", "msg00")
         msg01 = message(h0, gate01, 1, "msg01", "msg01")

@@ -52,12 +52,15 @@ def tile_picked_gatedg_relu_e_kernel(tc, xT, w1, w2, w3, offs, cen, pos1, pos2, 
             nc.sync.dma_start(raw[:], w.rearrange("(p j) n -> p j n", j=4)[:, :, c0:c1])
             return raw
 
+        def round_into(copy, grouped, raw):
+            copy(
+                grouped.rearrange("p (c i j) -> p c j i", i=RUN, j=4),
+                raw.rearrange("p j (c i) -> p c j i", i=RUN),
+            )
+
         def round_weight(copy, raw, name, tag, c0=0):
             grouped = keep.tile([P, P * 4], BF16, name=name, tag=tag, align_bytes=ALIGN)
-            copy(
-                grouped[:].rearrange("p (c i j) -> p c j i", i=RUN, j=4),
-                raw[:, :, c0 : c0 + P].rearrange("p j (c i) -> p c j i", i=RUN),
-            )
+            round_into(copy, grouped[:], raw[:, :, c0 : c0 + P])
             return grouped
 
         def code_tiles(width, name, tag):
@@ -120,10 +123,9 @@ def tile_picked_gatedg_relu_e_kernel(tc, xT, w1, w2, w3, offs, cen, pos1, pos2, 
         for j in range(1, 4):
             load_plane(j)
         w10_raw = load_weight(w1, 0, P, "w10_raw")
-        w20_raw = load_weight(w2, 0, P, "w20_raw")
+        w2_raw = load_weight(w2, 0, N, "w2_raw")
         w11_raw = load_weight(w1, P, N, "w11_raw")
         cen_t = load_list(cen, "cen_t")
-        w21_raw = load_weight(w2, P, N, "w21_raw")
         pos_t = [load_list(pos1, "pos1_t"), load_list(pos2, "pos2_t")]
         w3_raw = load_weight(w3, 0, N, "w3_raw")
 
@@ -133,7 +135,9 @@ def tile_picked_gatedg_relu_e_kernel(tc, xT, w1, w2, w3, offs, cen, pos1, pos2, 
             gather_plane(j)
 
         w10_bf = round_weight(nc.vector.tensor_copy, w10_raw, "w10_bf", "w10_bf")
-        w20_bf = round_weight(nc.scalar.copy, w20_raw, "w20_bf", "w20_bf")
+        w20_bf = round_weight(nc.scalar.copy, w2_raw, "w20_bf", "w20_bf")
+        late_bf = keep.tile([P, N * 4], BF16, name="late_bf", align_bytes=ALIGN)
+        round_into(nc.scalar.copy, late_bf[:, P * 4 :], w2_raw[:, :, P:N])
         x_first_q = code_tiles(HALF, "x_first", "x_first_codes")
         quantize_columns(x_first_q, x_first, 0, QUARTER)
         w10_q = quantize(w10_bf, (P,), "w10", "w10_codes")
@@ -141,7 +145,7 @@ def tile_picked_gatedg_relu_e_kernel(tc, xT, w1, w2, w3, offs, cen, pos1, pos2, 
         x_second_q = quantize(x_second, (QUARTER, P, P), "x_second", "x_second_codes")
         x_q = [x_first_q, x_second_q]
         w20_q = quantize(w20_bf, (P,), "w20", "w20_codes")
-        w11_bf = round_weight(nc.vector.tensor_copy, w11_raw, "w11_bf", "w11_bf")
+        round_into(nc.vector.tensor_copy, late_bf[:, : P * 4], w11_raw[:])
 
         def product(w_q, name, tag, pieces):
             rows = keep.tile([P, S], F32, name=name, tag=tag, align_bytes=ALIGN)
@@ -153,8 +157,8 @@ def tile_picked_gatedg_relu_e_kernel(tc, xT, w1, w2, w3, offs, cen, pos1, pos2, 
                     nodes = slice(c0 - half * HALF + lo, c0 - half * HALF + lo + width)
                     nc.tensor.matmul_mx(
                         out=acc[:, lo : lo + width],
-                        lhsT=w_q[0][:].bitcast(FP8X4),
-                        lhsT_scale=w_q[1][:],
+                        lhsT=w_q[0].bitcast(FP8X4),
+                        lhsT_scale=w_q[1],
                         rhs=x_q[half][0][:, nodes].bitcast(FP8X4),
                         rhs_scale=x_q[half][1][:, nodes],
                         start=True,
@@ -165,6 +169,9 @@ def tile_picked_gatedg_relu_e_kernel(tc, xT, w1, w2, w3, offs, cen, pos1, pos2, 
 
         def halves(turn):
             return [(half * HALF, (half + 1) * HALF, (2 * turn + half) % RING, nc.scalar.copy, 1) for half in range(2)]
+
+        def block_of(quantized, block=0):
+            return [part[:, block * P : (block + 1) * P] for part in quantized]
 
         def entries(lst, c0, c1):
             return lst[:, c0 // PER_COLUMN : c1 // PER_COLUMN]
@@ -238,28 +245,28 @@ def tile_picked_gatedg_relu_e_kernel(tc, xT, w1, w2, w3, offs, cen, pos1, pos2, 
         y0_pieces = [
             (0, HALF, RING, nc.scalar.copy, 2),
             (HALF, HALF + QUARTER, RING + 1, nc.scalar.copy, 1),
-            (HALF + QUARTER, S - P, RING + 2, nc.scalar.copy, 1),
-            (S - P, S, RING + 3, nc.vector.tensor_copy, 1),
+            (HALF + QUARTER, S, RING + 2, nc.vector.tensor_copy, 2),
         ]
-        y0 = product(w10_q, "y0", "y0", y0_pieces)
-        w11_q = quantize(w11_bf, (P,), "w11", "w10_codes")
+        y0 = product(block_of(w10_q), "y0", "y0", y0_pieces)
+        late_q = quantize(late_bf, (N,), "late", "w10_codes")
         yc0 = centres(y0, "yc0", parts=2)
-        e0 = product(w20_q, "e0", "e0", halves(0))
+        e0_pieces = [(q * QUARTER, (q + 1) * QUARTER, q, nc.scalar.copy, 1) for q in range(4)]
+        e0 = product(block_of(w20_q), "e0", "e0", e0_pieces)
         pre00 = gate_input(yc0, e0, 0, "pre00", "pre00", parts=2)
-        w21_q = quantize(round_weight(nc.scalar.copy, w21_raw, "w21_bf", "w20_codes"), (P,), "w21", "w21_codes")
-        pre01 = gate_input(yc0, e0, 1, "pre01", "w21_raw")
-        y1 = product(w11_q, "y1", "y1", halves(1))
+        pre01 = gate_input(yc0, e0, 1, "pre01", "pre01")
+        y1 = product(block_of(late_q, 0), "y1", "y1", halves(0))
         yc1 = centres(y1, "yc1")
-        w30_q = quantize(round_weight(nc.scalar.copy, w3_raw, "w30_bf", "w10_codes"), (P,), "w30", "w30_codes")
-        e1 = product(w21_q, "e1", "e1", halves(2))
-        pre10 = gate_input(yc1, e1, 0, "pre10", "pre10")
+        e1 = product(block_of(late_q, 1), "e1", "e1", halves(1))
+        w3_bf = keep.tile([P, N * 4], BF16, name="w3_bf", tag="w10_codes", align_bytes=ALIGN)
+        round_into(nc.scalar.copy, w3_bf[:], w3_raw[:])
+        w3_q = quantize(w3_bf, (N,), "w3", "w3_codes")
         gate00 = sigmoid(pre00, "gate00")
-        w31_q = quantize(round_weight(nc.scalar.copy, w3_raw, "w31_bf", "w21_codes", P), (P,), "w31", "w31_codes")
-        pre11 = gate_input(yc1, e1, 1, "pre11", "w3_raw")
-        h0 = product(w30_q, "h0", "h0", halves(3))
+        pre10 = gate_input(yc1, e1, 0, "pre10", "pre00")
         gate01 = sigmoid(pre01, "gate01")
-        h1 = product(w31_q, "h1", "h1", halves(4))
+        pre11 = gate_input(yc1, e1, 1, "pre11", "pre01")
+        h0 = product(block_of(w3_q, 0), "h0", "h0", halves(2))
         gate10 = sigmoid(pre10, "gate10")
+        h1 = product(block_of(w3_q, 1), "h1", "h1", halves(3))
         gate11 = sigmoid(pre11, "gate11")
         msg00 = message(h0, gate00, 0, "msg00", "msg00")
         msg01 = message(h0, gate01, 1, "msg01", "msg01")

@@ -24,7 +24,7 @@ ALIGN = 256
 
 LOADS = ((4096,), (4096,), (2048, 2048), (2048, 1536, 512))
 SHARED = (2, 3)
-VECTOR_THIRDS = 2
+SCALAR_COLUMNS = 512
 RING = 3
 
 
@@ -98,11 +98,8 @@ def tile_picked_gatedg_relu_e_kernel(tc, xT, w1, w2, w3, offs, cen, pos1, pos2, 
         def round_plane(j):
             c0 = 0
             for width in LOADS[j]:
-                cut = c0 + width * VECTOR_THIRDS // 3 // 16 * 16
-                if c0 + width == T and j == 3:
-                    cut = c0 + width // 2
-                if cut > c0:
-                    nc.vector.tensor_copy(rounded[j][:, c0:cut], planes[j][:, c0:cut])
+                cut = c0 + width - min(SCALAR_COLUMNS, width // 2)
+                nc.vector.tensor_copy(rounded[j][:, c0:cut], planes[j][:, c0:cut])
                 nc.scalar.copy(rounded[j][:, cut : c0 + width], planes[j][:, cut : c0 + width])
                 c0 = c0 + width
 
@@ -206,18 +203,19 @@ def tile_picked_gatedg_relu_e_kernel(tc, xT, w1, w2, w3, offs, cen, pos1, pos2, 
 
         def finish_on_tensor(block, msgs, parts):
             width = V // parts
+            turned = [psum.tile([P, width], F32, name="turned%d" % i, tag="bank%d" % (RING + i)) for i in range(parts)]
             turned_relu = []
-            for i in range(parts):
-                turned = psum.tile([P, width], F32, name="turned", tag="bank%d" % (RING + i))
-                steps = [(msg, c0) for msg in msgs for c0 in range(0, width, P)]
-                for n, (msg, c0) in enumerate(steps):
-                    nc.tensor.matmul(
-                        turned[:, c0 : c0 + P], lhsT=msg[:, i * width + c0 : i * width + c0 + P], rhs=identity[:],
-                        is_transpose=True, start=(n == 0), stop=(n == len(steps) - 1),
-                    )
-                part = keep.tile([P, width], F32, name="turned_relu%d" % i, align_bytes=ALIGN)
-                nc.scalar.activation(part[:], turned[:], ACT.Relu)
-                turned_relu.append(part)
+            for d, msg in enumerate(msgs):
+                for i in range(parts):
+                    for c0 in range(0, width, P):
+                        nc.tensor.matmul(
+                            turned[i][:, c0 : c0 + P], lhsT=msg[:, i * width + c0 : i * width + c0 + P], rhs=identity[:],
+                            is_transpose=True, start=(d == 0 and c0 == 0), stop=(d == 1 and c0 == width - P),
+                        )
+                    if d == 1:
+                        part = keep.tile([P, width], F32, name="turned_relu%d" % i, align_bytes=ALIGN)
+                        nc.scalar.activation(part[:], turned[i][:], ACT.Relu)
+                        turned_relu.append(part)
             for i, part in enumerate(turned_relu):
                 back = psum.tile([P, width], F32, name="back", tag="bank%d" % (RING + parts + i))
                 for c0 in range(0, width, P):
@@ -256,20 +254,20 @@ def tile_picked_gatedg_relu_e_kernel(tc, xT, w1, w2, w3, offs, cen, pos1, pos2, 
         pre01 = gate_input(yc0, e0, 1, "pre01", "pre01")
         y1 = product(block_of(late_q, 0), "y1", "y1", halves(0))
         yc1 = centres(y1, "yc1")
-        e1 = product(block_of(late_q, 1), "e1", "e1", halves(1))
-        w3_bf = keep.tile([P, N * 4], BF16, name="w3_bf", tag="w10_codes", align_bytes=ALIGN)
+        w3_bf = keep.tile([P, N * 4], BF16, name="w3_bf", tag="w20_codes", align_bytes=ALIGN)
         round_into(nc.scalar.copy, w3_bf[:], w3_raw[:])
         w3_q = quantize(w3_bf, (N,), "w3", "w3_codes")
+        e1 = product(block_of(late_q, 1), "e1", "e1", halves(1))
+        pre10 = gate_input(yc1, e1, 0, "pre10", "pre10")
+        pre11 = gate_input(yc1, e1, 1, "pre11", "pre11")
         gate00 = sigmoid(pre00, "gate00")
-        pre10 = gate_input(yc1, e1, 0, "pre10", "pre00")
         gate01 = sigmoid(pre01, "gate01")
-        pre11 = gate_input(yc1, e1, 1, "pre11", "pre01")
         h0 = product(block_of(w3_q, 0), "h0", "h0", halves(2))
         gate10 = sigmoid(pre10, "gate10")
         h1 = product(block_of(w3_q, 1), "h1", "h1", halves(3))
         gate11 = sigmoid(pre11, "gate11")
         msg00 = message(h0, gate00, 0, "msg00", "msg00")
-        msg01 = message(h0, gate01, 1, "msg01", "msg01")
+        msg01 = message(h0, gate01, 1, "msg01", "msg01", parts=2)
         msg10 = message(h1, gate10, 0, "msg10", "msg10")
         finish_on_tensor(0, [msg00, msg01], 2)
         msg11 = message(h1, gate11, 1, "msg11", "msg11", parts=2)

@@ -131,14 +131,15 @@ def tile_picked_gatedg_relu_e_kernel(tc, xT, w1, w2, w3, offs, cen, pos1, pos2, 
                 round_plane(j)
             gather_plane(j)
 
-        w10_bf = round_weight(nc.vector.tensor_copy, w10_raw, "w10_bf", "w10_bf")
+        def round_on_gpsimd(dst, src):
+            nc.gpsimd.tensor_scalar(dst, src, 1.0, 0.0, ALU.mult, ALU.add)
+
+        w10_bf = round_weight(round_on_gpsimd, w10_raw, "w10_bf", "w10_bf")
         w20_bf = round_weight(nc.scalar.copy, w2_raw, "w20_bf", "w20_bf")
         late_bf = keep.tile([P, N * 4], BF16, name="late_bf", align_bytes=ALIGN)
         round_into(nc.scalar.copy, late_bf[:, P * 4 :], w2_raw[:, :, P:N])
-        x_first_q = code_tiles(HALF, "x_first", "x_first_codes")
-        quantize_columns(x_first_q, x_first, 0, QUARTER)
         w10_q = quantize(w10_bf, (P,), "w10", "w10_codes")
-        quantize_columns(x_first_q, x_first, QUARTER, HALF)
+        x_first_q = quantize(x_first, (QUARTER, QUARTER), "x_first", "w10_raw")
         x_second_q = quantize(x_second, (QUARTER, P, P), "x_second", "x_second_codes")
         x_q = [x_first_q, x_second_q]
         w20_q = quantize(w20_bf, (P,), "w20", "w20_codes")

@@ -242,9 +242,10 @@ def tile_picked_gatedg_relu_e_kernel(tc, xT, w1, w2, w3, offs, cen, pos1, pos2, 
                 nc.sync.dma_start(out[block * P : (block + 1) * P, i * width : (i + 1) * width], res[:])
 
         y0_pieces = [
-            (0, HALF, RING, nc.scalar.copy, 2),
-            (HALF, HALF + QUARTER, RING + 1, nc.scalar.copy, 1),
-            (HALF + QUARTER, S, RING + 2, nc.vector.tensor_copy, 2),
+            (0, QUARTER, RING, nc.scalar.copy, 1),
+            (QUARTER, HALF, RING + 1, nc.scalar.copy, 1),
+            (HALF, HALF + QUARTER, RING + 2, nc.scalar.copy, 1),
+            (HALF + QUARTER, S, RING + 3, nc.vector.tensor_copy, 2),
         ]
         y0 = product(block_of(w10_q), "y0", "y0", y0_pieces)
         late_q = quantize(late_bf, (N,), "late", "w10_codes")

@@ -137,12 +137,12 @@ def tile_picked_gatedg_relu_e_kernel(tc, xT, w1, w2, w3, offs, cen, pos1, pos2, 
         w10_bf = round_weight(round_on_gpsimd, w10_raw, "w10_bf", "w10_bf")
         w20_bf = round_weight(nc.scalar.copy, w2_raw, "w20_bf", "w20_bf")
         late_bf = keep.tile([P, N * 4], BF16, name="late_bf", align_bytes=ALIGN)
-        round_into(nc.scalar.copy, late_bf[:, P * 4 :], w2_raw[:, :, P:N])
         w10_q = quantize(w10_bf, (P,), "w10", "w10_codes")
         x_first_q = quantize(x_first, (QUARTER, QUARTER), "x_first", "w10_raw")
         x_second_q = quantize(x_second, (QUARTER, P, P), "x_second", "x_second_codes")
         x_q = [x_first_q, x_second_q]
         w20_q = quantize(w20_bf, (P,), "w20", "w20_codes")
+        round_into(nc.vector.tensor_copy, late_bf[:, P * 4 :], w2_raw[:, :, P:N])
         round_into(nc.vector.tensor_copy, late_bf[:, : P * 4], w11_raw[:])
 
         def product(w_q, name, tag, pieces):

@@ -18,6 +18,7 @@ ALU = mybir.AluOpType
 P = 128
 HALF = S // 2
 QUARTER = S // 4
+SIDE = V // 2
 PER_COLUMN = 16
 RUN = 4
 ALIGN = 256
@@ -25,7 +26,6 @@ ALIGN = 256
 LOADS = ((4096,), (4096,), (2048, 2048), (2048, 1536, 512))
 SHARED = (2, 3)
 SCALAR_COLUMNS = 512
-RING = 3
 
 
 def tile_picked_gatedg_relu_e_kernel(tc, xT, w1, w2, w3, offs, cen, pos1, pos2, out):
@@ -34,12 +34,18 @@ def tile_picked_gatedg_relu_e_kernel(tc, xT, w1, w2, w3, offs, cen, pos1, pos2, 
         keep = ctx.enter_context(tc.tile_pool(name="keep", bufs=1))
         psum = ctx.enter_context(tc.psum_pool(name="psum", bufs=1))
 
+        def sbuf(width, dtype, name, tag=None):
+            return keep.tile([P, width], dtype, name=name, tag=tag or name, align_bytes=ALIGN)
+
+        def bank(number, width):
+            return psum.tile([P, width], F32, name="bank", tag="bank%d" % number)
+
         warm_in = keep.tile([P, 8], F32, name="warm_in")
         warm_out = keep.tile([P, 8], F32, name="warm_out")
         nc.vector.memset(warm_in[:], 0.0)
         nc.scalar.activation(warm_out[:], warm_in[:], ACT.Sigmoid)
 
-        identity = keep.tile([P, P], F32, name="identity", align_bytes=ALIGN)
+        identity = sbuf(P, F32, "identity")
         make_identity(nc, identity[:])
 
         def load_list(src, name):
@@ -58,36 +64,35 @@ def tile_picked_gatedg_relu_e_kernel(tc, xT, w1, w2, w3, offs, cen, pos1, pos2, 
                 raw.rearrange("p j (c i) -> p c j i", i=RUN),
             )
 
-        def round_weight(copy, raw, name, tag, c0=0):
-            grouped = keep.tile([P, P * 4], BF16, name=name, tag=tag, align_bytes=ALIGN)
-            round_into(copy, grouped[:], raw[:, :, c0 : c0 + P])
+        def round_weight(copy, raw, name):
+            grouped = sbuf(4 * raw.shape[2], BF16, name)
+            round_into(copy, grouped[:], raw)
             return grouped
 
-        def code_tiles(width, name, tag):
-            codes = keep.tile([P, width], U32, name=name + "_codes", tag=tag, align_bytes=ALIGN)
-            scales = keep.tile([P, width], U8, name=name + "_scales", tag=name + "_scales", align_bytes=ALIGN)
-            return codes, scales
+        def round_on_gpsimd(dst, src):
+            nc.gpsimd.tensor_scalar(dst, src, 1.0, 0.0, ALU.mult, ALU.add)
 
-        def quantize_columns(quantized, grouped, c0, c1):
-            nc.vector.quantize_mx(
-                out=quantized[0][:, c0:c1].bitcast(FP8X4),
-                scales=quantized[1][:, c0:c1],
-                in_=grouped[:, 4 * c0 : 4 * c1],
-            )
-
-        def quantize(grouped, widths, name, tag):
-            quantized = code_tiles(sum(widths), name, tag)
+        def quantize(grouped, widths, name, tag=None):
+            codes = sbuf(sum(widths), U32, name + "_codes", tag)
+            scales = sbuf(sum(widths), U8, name + "_scales")
             c0 = 0
             for width in widths:
-                quantize_columns(quantized, grouped, c0, c0 + width)
+                nc.vector.quantize_mx(
+                    out=codes[:, c0 : c0 + width].bitcast(FP8X4),
+                    scales=scales[:, c0 : c0 + width],
+                    in_=grouped[:, 4 * c0 : 4 * (c0 + width)],
+                )
                 c0 = c0 + width
-            return quantized
+            return codes, scales
 
         x_rows = xT.rearrange("(p j) t -> p j t", j=4)
-        planes = [keep.tile([P, T], F32, name="plane%d" % j, align_bytes=ALIGN) for j in range(4)]
-        rounded = {j: keep.tile([P, T], BF16, name="rounded%d" % j, align_bytes=ALIGN) for j in SHARED}
-        x_first = keep.tile([P, 4 * HALF], BF16, name="x_first", tag="x_first", align_bytes=ALIGN)
-        x_second = keep.tile([P, 4 * HALF], BF16, name="x_second", tag="x_second", align_bytes=ALIGN)
+        planes = [sbuf(T, F32, "plane%d" % j) for j in range(4)]
+        rounded = {j: sbuf(T, BF16, "rounded%d" % j) for j in SHARED}
+        x_first = sbuf(4 * HALF, BF16, "x_first")
+        x_second = sbuf(4 * HALF, BF16, "x_second")
+
+        def entries(lst, c0, c1):
+            return lst[:, c0 // PER_COLUMN : c1 // PER_COLUMN]
 
         def load_plane(j):
             c0 = 0
@@ -104,16 +109,13 @@ def tile_picked_gatedg_relu_e_kernel(tc, xT, w1, w2, w3, offs, cen, pos1, pos2, 
                 c0 = c0 + width
 
         def gather_plane(j):
-            nc.vector.tensor_copy(
-                x_first[:].rearrange("p (n j) -> p n j", j=4)[:, :, j],
-                planes[j][:].indirect(offs_t[:, 0 : HALF // PER_COLUMN]),
-            )
+            first = x_first[:].rearrange("p (n j) -> p n j", j=4)[:, :, j]
             second = x_second[:].rearrange("p (n j) -> p n j", j=4)[:, :, j]
-            second_entries = offs_t[:, HALF // PER_COLUMN : S // PER_COLUMN]
+            nc.vector.tensor_copy(first, planes[j][:].indirect(entries(offs_t, 0, HALF)))
             if j in SHARED:
-                nc.scalar.activation(second, rounded[j][:].indirect(second_entries), ACT.Copy)
+                nc.scalar.activation(second, rounded[j][:].indirect(entries(offs_t, HALF, S)), ACT.Copy)
             else:
-                nc.vector.tensor_copy(second, planes[j][:].indirect(second_entries))
+                nc.vector.tensor_copy(second, planes[j][:].indirect(entries(offs_t, HALF, S)))
 
         load_plane(0)
         offs_t = load_list(offs, "offs_t")
@@ -123,154 +125,143 @@ def tile_picked_gatedg_relu_e_kernel(tc, xT, w1, w2, w3, offs, cen, pos1, pos2, 
         w2_raw = load_weight(w2, 0, N, "w2_raw")
         w11_raw = load_weight(w1, P, N, "w11_raw")
         cen_t = load_list(cen, "cen_t")
-        pos_t = [load_list(pos1, "pos1_t"), load_list(pos2, "pos2_t")]
         w3_raw = load_weight(w3, 0, N, "w3_raw")
+        pos_t = [load_list(pos1, "pos1_t"), load_list(pos2, "pos2_t")]
 
         for j in range(4):
             if j in SHARED:
                 round_plane(j)
             gather_plane(j)
 
-        def round_on_gpsimd(dst, src):
-            nc.gpsimd.tensor_scalar(dst, src, 1.0, 0.0, ALU.mult, ALU.add)
+        w10_bf = round_weight(round_on_gpsimd, w10_raw[:], "w10_bf")
+        w20_bf = round_weight(nc.scalar.copy, w2_raw[:, :, 0:P], "w20_bf")
+        w10_q = quantize(w10_bf, (P,), "w10")
+        x_q = [
+            quantize(x_first, (QUARTER, QUARTER), "x_first", "w10_raw"),
+            quantize(x_second, (QUARTER, P, P), "x_second"),
+        ]
+        w20_q = quantize(w20_bf, (P,), "w20")
+        late_bf = sbuf(4 * N, BF16, "late_bf")
+        round_into(nc.vector.tensor_copy, late_bf[:, 4 * P :], w2_raw[:, :, P:N])
+        round_into(nc.vector.tensor_copy, late_bf[:, : 4 * P], w11_raw[:])
+        w30_bf = round_weight(nc.vector.tensor_copy, w3_raw[:, :, 0:P], "w30_bf")
+        late_q = quantize(late_bf, (N,), "late")
+        w31_bf = round_weight(nc.vector.tensor_copy, w3_raw[:, :, P:N], "w31_bf")
+        w30_q = quantize(w30_bf, (P,), "w30")
 
-        w10_bf = round_weight(round_on_gpsimd, w10_raw, "w10_bf", "w10_bf")
-        w20_bf = round_weight(nc.scalar.copy, w2_raw, "w20_bf", "w20_bf")
-        late_bf = keep.tile([P, N * 4], BF16, name="late_bf", align_bytes=ALIGN)
-        w10_q = quantize(w10_bf, (P,), "w10", "w10_codes")
-        x_first_q = quantize(x_first, (QUARTER, QUARTER), "x_first", "w10_raw")
-        x_second_q = quantize(x_second, (QUARTER, P, P), "x_second", "x_second_codes")
-        x_q = [x_first_q, x_second_q]
-        w20_q = quantize(w20_bf, (P,), "w20", "w20_codes")
-        round_into(nc.vector.tensor_copy, late_bf[:, P * 4 :], w2_raw[:, :, P:N])
-        round_into(nc.vector.tensor_copy, late_bf[:, : P * 4], w11_raw[:])
+        def product(w_q, block, rows, c0, c1, number, copy, parts=1):
+            half = c0 // HALF
+            acc = bank(number, c1 - c0)
+            width = (c1 - c0) // parts
+            columns = slice(block * P, (block + 1) * P)
+            for lo in range(0, c1 - c0, width):
+                nodes = slice(c0 - half * HALF + lo, c0 - half * HALF + lo + width)
+                nc.tensor.matmul_mx(
+                    out=acc[:, lo : lo + width],
+                    lhsT=w_q[0][:, columns].bitcast(FP8X4),
+                    lhsT_scale=w_q[1][:, columns],
+                    rhs=x_q[half][0][:, nodes].bitcast(FP8X4),
+                    rhs_scale=x_q[half][1][:, nodes],
+                    start=True,
+                    stop=True,
+                )
+            copy(rows[:, c0:c1], acc[:])
 
-        def product(w_q, name, tag, pieces):
-            rows = keep.tile([P, S], F32, name=name, tag=tag, align_bytes=ALIGN)
-            for c0, c1, bank, copy, parts in pieces:
-                half = c0 // HALF
-                acc = psum.tile([P, c1 - c0], F32, name="acc", tag="bank%d" % bank)
-                width = (c1 - c0) // parts
-                for lo in range(0, c1 - c0, width):
-                    nodes = slice(c0 - half * HALF + lo, c0 - half * HALF + lo + width)
-                    nc.tensor.matmul_mx(
-                        out=acc[:, lo : lo + width],
-                        lhsT=w_q[0].bitcast(FP8X4),
-                        lhsT_scale=w_q[1],
-                        rhs=x_q[half][0][:, nodes].bitcast(FP8X4),
-                        rhs_scale=x_q[half][1][:, nodes],
-                        start=True,
-                        stop=True,
-                    )
-                copy(rows[:, c0:c1], acc[:])
+        def product_in_halves(w_q, block, name, first_bank):
+            rows = sbuf(S, F32, name)
+            for half in range(2):
+                product(w_q, block, rows, half * HALF, (half + 1) * HALF, first_bank + half, nc.scalar.copy)
             return rows
 
-        def halves(turn):
-            return [(half * HALF, (half + 1) * HALF, (2 * turn + half) % RING, nc.scalar.copy, 1) for half in range(2)]
+        def centres(yc, y, c0, c1):
+            nc.scalar.activation(yc[:, c0:c1], y[:].indirect(entries(cen_t, c0, c1)), ACT.Copy)
 
-        def block_of(quantized, block=0):
-            return [part[:, block * P : (block + 1) * P] for part in quantized]
-
-        def entries(lst, c0, c1):
-            return lst[:, c0 // PER_COLUMN : c1 // PER_COLUMN]
-
-        def centres(y, name, parts=1):
-            yc = keep.tile([P, V], F32, name=name, align_bytes=ALIGN)
-            width = V // parts
-            for c0 in range(0, V, width):
-                nc.vector.tensor_copy(yc[:, c0 : c0 + width], y[:].indirect(entries(cen_t, c0, c0 + width)))
-            return yc
-
-        def gate_input(yc, e, d, name, tag, parts=1):
-            pre = keep.tile([P, V], F32, name=name, tag=tag, align_bytes=ALIGN)
-            width = V // parts
-            for c0 in range(0, V, width):
-                cols = slice(c0, c0 + width)
-                nc.vector.tensor_tensor(pre[:, cols], e[:].indirect(entries(pos_t[d], c0, c0 + width)), yc[:, cols], ALU.add)
-            return pre
+        def neighbours(dst, rows, d, c0, c1, other, op):
+            nc.vector.tensor_tensor(dst, rows[:].indirect(entries(pos_t[d], c0, c1)), other, op)
 
         def sigmoid(pre, name):
-            gate = keep.tile([P, V], F32, name=name, tag=name, align_bytes=ALIGN)
+            gate = sbuf(V, F32, name)
             nc.scalar.activation(gate[:], pre[:], ACT.Sigmoid)
             return gate
 
-        def message(h, gate, d, name, tag, parts=1):
-            msg = keep.tile([P, V], F32, name=name, tag=tag, align_bytes=ALIGN)
-            width = V // parts
-            for c0 in range(0, V, width):
-                cols = slice(c0, c0 + width)
-                nc.vector.tensor_tensor(msg[:, cols], h[:].indirect(entries(pos_t[d], c0, c0 + width)), gate[:, cols], ALU.mult)
-            return msg
-
-        def finish_on_tensor(block, msgs, parts):
-            width = V // parts
-            turned = [psum.tile([P, width], F32, name="turned%d" % i, tag="bank%d" % (RING + i)) for i in range(parts)]
-            turned_relu = []
+        def sum_turned(msgs, number):
+            width = msgs[0].shape[1]
+            turned = bank(number, width)
             for d, msg in enumerate(msgs):
-                for i in range(parts):
-                    for c0 in range(0, width, P):
-                        nc.tensor.matmul(
-                            turned[i][:, c0 : c0 + P], lhsT=msg[:, i * width + c0 : i * width + c0 + P], rhs=identity[:],
-                            is_transpose=True, start=(d == 0 and c0 == 0), stop=(d == 1 and c0 == width - P),
-                        )
-                    if d == 1:
-                        part = keep.tile([P, width], F32, name="turned_relu%d" % i, align_bytes=ALIGN)
-                        nc.scalar.activation(part[:], turned[i][:], ACT.Relu)
-                        turned_relu.append(part)
-            for i, part in enumerate(turned_relu):
-                back = psum.tile([P, width], F32, name="back", tag="bank%d" % (RING + parts + i))
                 for c0 in range(0, width, P):
-                    nc.tensor.transpose(back[:, c0 : c0 + P], part[:, c0 : c0 + P], identity[:])
-                res = keep.tile([P, width], F32, name="res%d_%d" % (block, i))
-                nc.scalar.copy(res[:], back[:])
-                nc.sync.dma_start(out[block * P : (block + 1) * P, i * width : (i + 1) * width], res[:])
+                    nc.tensor.matmul(
+                        turned[:, c0 : c0 + P], lhsT=msg[:, c0 : c0 + P], rhs=identity[:],
+                        is_transpose=True, start=(d == 0 and c0 == 0), stop=(d == 1 and c0 == width - P),
+                    )
+            return turned
 
-        def relu_on_vector(res, total):
-            nc.vector.tensor_scalar_max(res, total, 0.0)
+        def relu_turned(turned, name):
+            part = sbuf(turned.shape[1], F32, name)
+            nc.scalar.activation(part[:], turned[:], ACT.Relu)
+            return part
 
-        def finish(block, msgs, tags, relu):
-            width = V // len(tags)
-            totals = []
-            for i, tag in enumerate(tags):
-                cols = slice(i * width, (i + 1) * width)
-                total = keep.tile([P, width], F32, name="total%d_%d" % (block, i), tag=tag, align_bytes=ALIGN)
-                nc.vector.tensor_tensor(total[:], msgs[0][:, cols], msgs[1][:, cols], ALU.add)
-                totals.append(total)
-            for i, total in enumerate(totals):
-                res = keep.tile([P, width], F32, name="res%d_%d" % (block, i))
-                relu(res[:], total[:])
-                nc.sync.dma_start(out[block * P : (block + 1) * P, i * width : (i + 1) * width], res[:])
+        def turn_back_and_store(part, number, block, v0, name):
+            width = part.shape[1]
+            back = bank(number, width)
+            for c0 in range(0, width, P):
+                nc.tensor.transpose(back[:, c0 : c0 + P], part[:, c0 : c0 + P], identity[:])
+            res = sbuf(width, F32, name)
+            nc.scalar.copy(res[:], back[:])
+            nc.sync.dma_start(out[block * P : (block + 1) * P, v0 : v0 + width], res[:])
 
-        y0_pieces = [
-            (0, QUARTER, RING, nc.scalar.copy, 1),
-            (QUARTER, HALF, RING + 1, nc.scalar.copy, 1),
-            (HALF, HALF + QUARTER, RING + 2, nc.scalar.copy, 1),
-            (HALF + QUARTER, S, RING + 3, nc.vector.tensor_copy, 2),
-        ]
-        y0 = product(block_of(w10_q), "y0", "y0", y0_pieces)
-        late_q = quantize(late_bf, (N,), "late", "w10_codes")
-        yc0 = centres(y0, "yc0", parts=2)
-        e0_pieces = [(q * QUARTER, (q + 1) * QUARTER, q, nc.scalar.copy, 1) for q in range(4)]
-        e0 = product(block_of(w20_q), "e0", "e0", e0_pieces)
-        pre00 = gate_input(yc0, e0, 0, "pre00", "pre00", parts=2)
-        pre01 = gate_input(yc0, e0, 1, "pre01", "pre01")
-        y1 = product(block_of(late_q, 0), "y1", "y1", halves(0))
-        yc1 = centres(y1, "yc1")
-        w3_bf = keep.tile([P, N * 4], BF16, name="w3_bf", tag="w20_codes", align_bytes=ALIGN)
-        round_into(nc.scalar.copy, w3_bf[:], w3_raw[:])
-        w3_q = quantize(w3_bf, (N,), "w3", "w3_codes")
-        e1 = product(block_of(late_q, 1), "e1", "e1", halves(1))
-        pre10 = gate_input(yc1, e1, 0, "pre10", "pre10")
-        pre11 = gate_input(yc1, e1, 1, "pre11", "pre11")
+        y0 = sbuf(S, F32, "y0")
+        e0 = sbuf(S, F32, "e0")
+        for q in range(4):
+            product(w10_q, 0, y0, q * QUARTER, (q + 1) * QUARTER, q, nc.scalar.copy, parts=2 if q == 3 else 1)
+        yc0 = sbuf(V, F32, "yc0")
+        for q in range(4):
+            product(w20_q, 0, e0, q * QUARTER, (q + 1) * QUARTER, 4 + q, nc.vector.tensor_copy if q in (1, 2) else nc.scalar.copy)
+            if q == 0:
+                centres(yc0, y0, 0, V)
+        w31_q = quantize(w31_bf, (P,), "w31")
+
+        pre00 = sbuf(V, F32, "pre00")
+        pre01 = sbuf(V, F32, "pre01")
+        neighbours(pre00[:], e0, 0, 0, V, yc0[:], ALU.add)
+        neighbours(pre01[:], e0, 1, 0, V, yc0[:], ALU.add)
+
+        y1 = product_in_halves(late_q, 0, "y1", 0)
+        h0 = product_in_halves(w30_q, 0, "h0", 2)
         gate00 = sigmoid(pre00, "gate00")
         gate01 = sigmoid(pre01, "gate01")
-        h0 = product(block_of(w3_q, 0), "h0", "h0", halves(2))
-        gate10 = sigmoid(pre10, "gate10")
-        h1 = product(block_of(w3_q, 1), "h1", "h1", halves(3))
-        gate11 = sigmoid(pre11, "gate11")
-        msg00 = message(h0, gate00, 0, "msg00", "msg00")
-        msg01 = message(h0, gate01, 1, "msg01", "msg01", parts=2)
-        msg10 = message(h1, gate10, 0, "msg10", "msg10")
-        finish_on_tensor(0, [msg00, msg01], 2)
-        msg11 = message(h1, gate11, 1, "msg11", "msg11", parts=2)
-        finish(1, [msg10, msg11], ["total_a", "total_b"], relu_on_vector)
+        msg00 = sbuf(V, F32, "msg00")
+        msg01 = sbuf(V, F32, "msg01")
+        neighbours(msg00[:], h0, 0, 0, V, gate00[:], ALU.mult)
+        neighbours(msg01[:], h0, 1, 0, V, gate01[:], ALU.mult)
+
+        e1 = product_in_halves(late_q, 1, "e1", 2)
+        yc1 = sbuf(V, F32, "yc1")
+        sides = [(0, SIDE), (SIDE, V)]
+        pre1 = []
+        for i, (c0, c1) in enumerate(sides):
+            centres(yc1, y1, c0, c1)
+            pre = sbuf(V, F32, "pre1_%d" % i)
+            for d in range(2):
+                neighbours(pre[:, d * SIDE : (d + 1) * SIDE], e1, d, c0, c1, yc1[:, c0:c1], ALU.add)
+            pre1.append(pre)
+        h1 = product_in_halves(w31_q, 0, "h1", 2)
+        gate1 = [sigmoid(pre1[0], "gate1_0")]
+        relu0 = relu_turned(sum_turned([msg00[:], msg01[:]], 6), "relu0")
+        gate1.append(sigmoid(pre1[1], "gate1_1"))
+        turn_back_and_store(relu0, 7, 0, 0, "res0")
+        msg1 = []
+        for i, (c0, c1) in enumerate(sides):
+            msg = sbuf(V, F32, "msg1_%d" % i)
+            for d in range(2):
+                cols = slice(d * SIDE, (d + 1) * SIDE)
+                neighbours(msg[:, cols], h1, d, c0, c1, gate1[i][:, cols], ALU.mult)
+            msg1.append(msg)
+
+        relu1 = relu_turned(sum_turned([msg1[0][:, :SIDE], msg1[0][:, SIDE:]], 0), "relu1")
+        turn_back_and_store(relu1, 1, 1, 0, "res1")
+
+        total = sbuf(SIDE, F32, "total")
+        nc.vector.tensor_tensor(total[:], msg1[1][:, :SIDE], msg1[1][:, SIDE:], ALU.add)
+        res = sbuf(SIDE, F32, "res")
+        nc.vector.tensor_scalar_max(res[:], total[:], 0.0)
+        nc.sync.dma_start(out[P:N, SIDE:V], res[:])

@@ -142,7 +142,7 @@ def tile_picked_gatedg_relu_e_kernel(tc, xT, w1, w2, w3, offs, cen, pos1, pos2, 
         ]
         w20_q = quantize(w20_bf, (P,), "w20")
         late_bf = sbuf(4 * N, BF16, "late_bf")
-        round_into(nc.vector.tensor_copy, late_bf[:, 4 * P :], w2_raw[:, :, P:N])
+        round_into(nc.scalar.copy, late_bf[:, 4 * P :], w2_raw[:, :, P:N])
         round_into(nc.vector.tensor_copy, late_bf[:, : 4 * P], w11_raw[:])
         w30_bf = round_weight(nc.vector.tensor_copy, w3_raw[:, :, 0:P], "w30_bf")
         late_q = quantize(late_bf, (N,), "late")
@@ -236,32 +236,34 @@ def tile_picked_gatedg_relu_e_kernel(tc, xT, w1, w2, w3, offs, cen, pos1, pos2, 
 
         e1 = product_in_halves(late_q, 1, "e1", 2)
         yc1 = sbuf(V, F32, "yc1")
+        pre10 = sbuf(V, F32, "pre10")
+        pre11 = sbuf(V, F32, "pre11")
         sides = [(0, SIDE), (SIDE, V)]
-        pre1 = []
-        for i, (c0, c1) in enumerate(sides):
+        for c0, c1 in sides:
             centres(yc1, y1, c0, c1)
-            pre = sbuf(V, F32, "pre1_%d" % i)
-            for d in range(2):
-                neighbours(pre[:, d * SIDE : (d + 1) * SIDE], e1, d, c0, c1, yc1[:, c0:c1], ALU.add)
-            pre1.append(pre)
+            neighbours(pre10[:, c0:c1], e1, 0, c0, c1, yc1[:, c0:c1], ALU.add)
+        neighbours(pre11[:], e1, 1, 0, V, yc1[:], ALU.add)
         h1 = product_in_halves(w31_q, 0, "h1", 2)
-        gate1 = [sigmoid(pre1[0], "gate1_0")]
-        relu0 = relu_turned(sum_turned([msg00[:], msg01[:]], 6), "relu0")
-        gate1.append(sigmoid(pre1[1], "gate1_1"))
-        turn_back_and_store(relu0, 7, 0, 0, "res0")
-        msg1 = []
+        gate10 = sigmoid(pre10, "gate10")
+        fetched = sbuf(SIDE, F32, "fetched")
+        nc.scalar.activation(fetched[:], h1[:].indirect(entries(pos_t[1], SIDE, V)), ACT.Copy)
+        gate11 = sigmoid(pre11, "gate11")
+        turned = [sum_turned([msg00[:, c0:c1], msg01[:, c0:c1]], 2 + i) for i, (c0, c1) in enumerate(sides)]
+        relus = [relu_turned(part, "relu%d" % i) for i, part in enumerate(turned)]
         for i, (c0, c1) in enumerate(sides):
-            msg = sbuf(V, F32, "msg1_%d" % i)
-            for d in range(2):
-                cols = slice(d * SIDE, (d + 1) * SIDE)
-                neighbours(msg[:, cols], h1, d, c0, c1, gate1[i][:, cols], ALU.mult)
-            msg1.append(msg)
+            turn_back_and_store(relus[i], 4 + i, 0, c0, "res0_%d" % i)
 
-        relu1 = relu_turned(sum_turned([msg1[0][:, :SIDE], msg1[0][:, SIDE:]], 0), "relu1")
-        turn_back_and_store(relu1, 1, 1, 0, "res1")
-
-        total = sbuf(SIDE, F32, "total")
-        nc.vector.tensor_tensor(total[:], msg1[1][:, :SIDE], msg1[1][:, SIDE:], ALU.add)
-        res = sbuf(SIDE, F32, "res")
-        nc.vector.tensor_scalar_max(res[:], total[:], 0.0)
-        nc.sync.dma_start(out[P:N, SIDE:V], res[:])
+        msg10 = sbuf(V, F32, "msg10")
+        msg11 = sbuf(V, F32, "msg11")
+        neighbours(msg10[:], h1, 0, 0, V, gate10[:], ALU.mult)
+        neighbours(msg11[:, :SIDE], h1, 1, 0, SIDE, gate11[:, :SIDE], ALU.mult)
+        nc.vector.tensor_tensor(msg11[:, SIDE:], fetched[:], gate11[:, SIDE:], ALU.mult)
+        totals = []
+        for i, (c0, c1) in enumerate(sides):
+            total = sbuf(SIDE, F32, "total%d" % i)
+            nc.vector.tensor_tensor(total[:], msg10[:, c0:c1], msg11[:, c0:c1], ALU.add)
+            totals.append(total)
+        for i, (c0, c1) in enumerate(sides):
+            res = sbuf(SIDE, F32, "res1_%d" % i)
+            nc.vector.tensor_scalar_max(res[:], totals[i][:], 0.0)
+            nc.sync.dma_start(out[P:N, c0:c1], res[:])

@@ -64,8 +64,8 @@ def tile_picked_gatedg_relu_e_kernel(tc, xT, w1, w2, w3, offs, cen, pos1, pos2, 
                 raw.rearrange("p j (c i) -> p c j i", i=RUN),
             )
 
-        def round_weight(copy, raw, name):
-            grouped = sbuf(4 * raw.shape[2], BF16, name)
+        def round_weight(copy, raw, name, tag=None):
+            grouped = sbuf(4 * raw.shape[2], BF16, name, tag)
             round_into(copy, grouped[:], raw)
             return grouped
 
@@ -123,9 +123,10 @@ def tile_picked_gatedg_relu_e_kernel(tc, xT, w1, w2, w3, offs, cen, pos1, pos2, 
             load_plane(j)
         w10_raw = load_weight(w1, 0, P, "w10_raw")
         w2_raw = load_weight(w2, 0, N, "w2_raw")
+        w30_raw = load_weight(w3, 0, P, "w30_raw")
         w11_raw = load_weight(w1, P, N, "w11_raw")
         cen_t = load_list(cen, "cen_t")
-        w3_raw = load_weight(w3, 0, N, "w3_raw")
+        w31_raw = load_weight(w3, P, N, "w31_raw")
         pos_t = [load_list(pos1, "pos1_t"), load_list(pos2, "pos2_t")]
 
         for j in range(4):
@@ -142,12 +143,12 @@ def tile_picked_gatedg_relu_e_kernel(tc, xT, w1, w2, w3, offs, cen, pos1, pos2, 
         ]
         w20_q = quantize(w20_bf, (P,), "w20")
         late_bf = sbuf(4 * N, BF16, "late_bf")
-        round_into(nc.scalar.copy, late_bf[:, 4 * P :], w2_raw[:, :, P:N])
+        round_into(nc.vector.tensor_copy, late_bf[:, 4 * P :], w2_raw[:, :, P:N])
+        w30_bf = round_weight(nc.vector.tensor_copy, w30_raw[:], "w30_bf")
         round_into(nc.vector.tensor_copy, late_bf[:, : 4 * P], w11_raw[:])
-        w30_bf = round_weight(nc.vector.tensor_copy, w3_raw[:, :, 0:P], "w30_bf")
-        late_q = quantize(late_bf, (N,), "late")
-        w31_bf = round_weight(nc.vector.tensor_copy, w3_raw[:, :, P:N], "w31_bf")
         w30_q = quantize(w30_bf, (P,), "w30")
+        late_q = quantize(late_bf, (N,), "late")
+        w31_bf = round_weight(round_on_gpsimd, w31_raw[:], "w31_bf", "late_bf")
 
         def product(w_q, block, rows, c0, c1, number, copy, parts=1):
             half = c0 // HALF
@@ -215,7 +216,7 @@ def tile_picked_gatedg_relu_e_kernel(tc, xT, w1, w2, w3, offs, cen, pos1, pos2, 
             product(w10_q, 0, y0, q * QUARTER, (q + 1) * QUARTER, q, nc.scalar.copy, parts=2 if q == 3 else 1)
         yc0 = sbuf(V, F32, "yc0")
         for q in range(4):
-            product(w20_q, 0, e0, q * QUARTER, (q + 1) * QUARTER, 4 + q, nc.vector.tensor_copy if q in (1, 2) else nc.scalar.copy)
+            product(w20_q, 0, e0, q * QUARTER, (q + 1) * QUARTER, 4 + q, nc.vector.tensor_copy if q > 0 else nc.scalar.copy)
             if q == 0:
                 centres(yc0, y0, 0, V)
         w31_q = quantize(w31_bf, (P,), "w31")
@@ -225,9 +226,11 @@ def tile_picked_gatedg_relu_e_kernel(tc, xT, w1, w2, w3, offs, cen, pos1, pos2, 
         neighbours(pre00[:], e0, 0, 0, V, yc0[:], ALU.add)
         neighbours(pre01[:], e0, 1, 0, V, yc0[:], ALU.add)
 
-        y1 = product_in_halves(late_q, 0, "y1", 0)
-        h0 = product_in_halves(w30_q, 0, "h0", 2)
+        h0 = product_in_halves(w30_q, 0, "h0", 0)
+        y1 = sbuf(S, F32, "y1")
+        product(late_q, 0, y1, 0, HALF, 2, nc.scalar.copy)
         gate00 = sigmoid(pre00, "gate00")
+        product(late_q, 0, y1, HALF, S, 3, nc.scalar.copy)
         gate01 = sigmoid(pre01, "gate01")
         msg00 = sbuf(V, F32, "msg00")
         msg01 = sbuf(V, F32, "msg01")

@@ -142,36 +142,32 @@ def tile_picked_gatedg_relu_e_kernel(tc, xT, w1, w2, w3, offs, cen, pos1, pos2, 
             quantize(x_second, (QUARTER, P, P), "x_second"),
         ]
         w20_q = quantize(w20_bf, (P,), "w20")
-        late_bf = sbuf(4 * N, BF16, "late_bf")
-        round_into(nc.vector.tensor_copy, late_bf[:, 4 * P :], w2_raw[:, :, P:N])
+        w21_bf = round_weight(nc.vector.tensor_copy, w2_raw[:, :, P:N], "w21_bf")
         w30_bf = round_weight(nc.vector.tensor_copy, w30_raw[:], "w30_bf")
-        round_into(nc.vector.tensor_copy, late_bf[:, : 4 * P], w11_raw[:])
+        w11_bf = round_weight(nc.vector.tensor_copy, w11_raw[:], "w11_bf")
         w30_q = quantize(w30_bf, (P,), "w30")
-        late_q = quantize(late_bf, (N,), "late")
-        w31_bf = round_weight(round_on_gpsimd, w31_raw[:], "w31_bf", "late_bf")
+        w11_q = quantize(w11_bf, (P,), "w11")
+        w31_bf = round_weight(round_on_gpsimd, w31_raw[:], "w31_bf", "w11_bf")
 
-        def product(w_q, block, rows, c0, c1, number, copy, parts=1):
+        def product(w_q, rows, c0, c1, number, copy):
             half = c0 // HALF
             acc = bank(number, c1 - c0)
-            width = (c1 - c0) // parts
-            columns = slice(block * P, (block + 1) * P)
-            for lo in range(0, c1 - c0, width):
-                nodes = slice(c0 - half * HALF + lo, c0 - half * HALF + lo + width)
-                nc.tensor.matmul_mx(
-                    out=acc[:, lo : lo + width],
-                    lhsT=w_q[0][:, columns].bitcast(FP8X4),
-                    lhsT_scale=w_q[1][:, columns],
-                    rhs=x_q[half][0][:, nodes].bitcast(FP8X4),
-                    rhs_scale=x_q[half][1][:, nodes],
-                    start=True,
-                    stop=True,
-                )
+            nodes = slice(c0 - half * HALF, c1 - half * HALF)
+            nc.tensor.matmul_mx(
+                out=acc[:],
+                lhsT=w_q[0][:].bitcast(FP8X4),
+                lhsT_scale=w_q[1][:],
+                rhs=x_q[half][0][:, nodes].bitcast(FP8X4),
+                rhs_scale=x_q[half][1][:, nodes],
+                start=True,
+                stop=True,
+            )
             copy(rows[:, c0:c1], acc[:])
 
-        def product_in_halves(w_q, block, name, first_bank):
+        def product_in_halves(w_q, name, banks):
             rows = sbuf(S, F32, name)
             for half in range(2):
-                product(w_q, block, rows, half * HALF, (half + 1) * HALF, first_bank + half, nc.scalar.copy)
+                product(w_q, rows, half * HALF, (half + 1) * HALF, banks[half], nc.scalar.copy)
             return rows
 
         def centres(yc, y, c0, c1):
@@ -212,13 +208,15 @@ def tile_picked_gatedg_relu_e_kernel(tc, xT, w1, w2, w3, offs, cen, pos1, pos2, 
 
         y0 = sbuf(S, F32, "y0")
         e0 = sbuf(S, F32, "e0")
-        for q in range(4):
-            product(w10_q, 0, y0, q * QUARTER, (q + 1) * QUARTER, q, nc.scalar.copy, parts=2 if q == 3 else 1)
         yc0 = sbuf(V, F32, "yc0")
+        cuts = (0, QUARTER, HALF, HALF + QUARTER, S - P, S)
+        for i in range(5):
+            product(w10_q, y0, cuts[i], cuts[i + 1], i, nc.scalar.copy)
         for q in range(4):
-            product(w20_q, 0, e0, q * QUARTER, (q + 1) * QUARTER, 4 + q, nc.vector.tensor_copy if q > 0 else nc.scalar.copy)
+            product(w20_q, e0, q * QUARTER, (q + 1) * QUARTER, (5 + q) % 8, nc.vector.tensor_copy if q > 0 else nc.scalar.copy)
             if q == 0:
                 centres(yc0, y0, 0, V)
+        w21_q = quantize(w21_bf, (P,), "w21", "w20_codes")
         w31_q = quantize(w31_bf, (P,), "w31")
 
         pre00 = sbuf(V, F32, "pre00")
@@ -226,18 +224,18 @@ def tile_picked_gatedg_relu_e_kernel(tc, xT, w1, w2, w3, offs, cen, pos1, pos2, 
         neighbours(pre00[:], e0, 0, 0, V, yc0[:], ALU.add)
         neighbours(pre01[:], e0, 1, 0, V, yc0[:], ALU.add)
 
-        h0 = product_in_halves(w30_q, 0, "h0", 0)
+        h0 = product_in_halves(w30_q, "h0", (1, 4))
         y1 = sbuf(S, F32, "y1")
-        product(late_q, 0, y1, 0, HALF, 2, nc.scalar.copy)
+        product(w11_q, y1, 0, HALF, 2, nc.scalar.copy)
         gate00 = sigmoid(pre00, "gate00")
-        product(late_q, 0, y1, HALF, S, 3, nc.scalar.copy)
+        product(w11_q, y1, HALF, S, 3, nc.scalar.copy)
         gate01 = sigmoid(pre01, "gate01")
         msg00 = sbuf(V, F32, "msg00")
         msg01 = sbuf(V, F32, "msg01")
         neighbours(msg00[:], h0, 0, 0, V, gate00[:], ALU.mult)
         neighbours(msg01[:], h0, 1, 0, V, gate01[:], ALU.mult)
 
-        e1 = product_in_halves(late_q, 1, "e1", 2)
+        e1 = product_in_halves(w21_q, "e1", (2, 3))
         yc1 = sbuf(V, F32, "yc1")
         pre10 = sbuf(V, F32, "pre10")
         pre11 = sbuf(V, F32, "pre11")
@@ -246,7 +244,7 @@ def tile_picked_gatedg_relu_e_kernel(tc, xT, w1, w2, w3, offs, cen, pos1, pos2, 
             centres(yc1, y1, c0, c1)
             neighbours(pre10[:, c0:c1], e1, 0, c0, c1, yc1[:, c0:c1], ALU.add)
         neighbours(pre11[:], e1, 1, 0, V, yc1[:], ALU.add)
-        h1 = product_in_halves(w31_q, 0, "h1", 2)
+        h1 = product_in_halves(w31_q, "h1", (2, 3))
         gate10 = sigmoid(pre10, "gate10")
         fetched = sbuf(SIDE, F32, "fetched")
         nc.scalar.activation(fetched[:], h1[:].indirect(entries(pos_t[1], SIDE, V)), ACT.Copy)

@@ -224,18 +224,22 @@ def tile_picked_gatedg_relu_e_kernel(tc, xT, w1, w2, w3, offs, cen, pos1, pos2, 
         neighbours(pre00[:], e0, 0, 0, V, yc0[:], ALU.add)
         neighbours(pre01[:], e0, 1, 0, V, yc0[:], ALU.add)
 
-        h0 = product_in_halves(w30_q, "h0", (1, 4))
+        h0 = sbuf(S, F32, "h0")
+        for q in range(4):
+            product(w30_q, h0, q * QUARTER, (q + 1) * QUARTER, 1 + q, nc.scalar.copy)
         y1 = sbuf(S, F32, "y1")
-        product(w11_q, y1, 0, HALF, 2, nc.scalar.copy)
+        product(w11_q, y1, 0, HALF, 5, nc.scalar.copy)
         gate00 = sigmoid(pre00, "gate00")
-        product(w11_q, y1, HALF, S, 3, nc.scalar.copy)
+        product(w11_q, y1, HALF, S, 6, nc.scalar.copy)
+        e1 = sbuf(S, F32, "e1")
+        product(w21_q, e1, 0, HALF, 5, nc.scalar.copy)
         gate01 = sigmoid(pre01, "gate01")
+        product(w21_q, e1, HALF, S, 6, nc.scalar.copy)
         msg00 = sbuf(V, F32, "msg00")
         msg01 = sbuf(V, F32, "msg01")
         neighbours(msg00[:], h0, 0, 0, V, gate00[:], ALU.mult)
         neighbours(msg01[:], h0, 1, 0, V, gate01[:], ALU.mult)
 
-        e1 = product_in_halves(w21_q, "e1", (2, 3))
         yc1 = sbuf(V, F32, "yc1")
         pre10 = sbuf(V, F32, "pre10")
         pre11 = sbuf(V, F32, "pre11")
@@ -244,15 +248,15 @@ def tile_picked_gatedg_relu_e_kernel(tc, xT, w1, w2, w3, offs, cen, pos1, pos2, 
             centres(yc1, y1, c0, c1)
             neighbours(pre10[:, c0:c1], e1, 0, c0, c1, yc1[:, c0:c1], ALU.add)
         neighbours(pre11[:], e1, 1, 0, V, yc1[:], ALU.add)
-        h1 = product_in_halves(w31_q, "h1", (2, 3))
+        h1 = product_in_halves(w31_q, "h1", (5, 6))
         gate10 = sigmoid(pre10, "gate10")
         fetched = sbuf(SIDE, F32, "fetched")
         nc.scalar.activation(fetched[:], h1[:].indirect(entries(pos_t[1], SIDE, V)), ACT.Copy)
         gate11 = sigmoid(pre11, "gate11")
-        turned = [sum_turned([msg00[:, c0:c1], msg01[:, c0:c1]], 2 + i) for i, (c0, c1) in enumerate(sides)]
+        turned = [sum_turned([msg00[:, c0:c1], msg01[:, c0:c1]], 5 + i) for i, (c0, c1) in enumerate(sides)]
         relus = [relu_turned(part, "relu%d" % i) for i, part in enumerate(turned)]
         for i, (c0, c1) in enumerate(sides):
-            turn_back_and_store(relus[i], 4 + i, 0, c0, "res0_%d" % i)
+            turn_back_and_store(relus[i], 1 + i, 0, c0, "res0_%d" % i)
 
         msg10 = sbuf(V, F32, "msg10")
         msg11 = sbuf(V, F32, "msg11")

@@ -142,12 +142,16 @@ def tile_picked_gatedg_relu_e_kernel(tc, xT, w1, w2, w3, offs, cen, pos1, pos2, 
             quantize(x_second, (QUARTER, P, P), "x_second"),
         ]
         w20_q = quantize(w20_bf, (P,), "w20")
-        w21_bf = round_weight(nc.vector.tensor_copy, w2_raw[:, :, P:N], "w21_bf")
+        late_bf = sbuf(4 * N, BF16, "late_bf")
+        round_into(nc.vector.tensor_copy, late_bf[:, 4 * P :], w2_raw[:, :, P:N])
         w30_bf = round_weight(nc.vector.tensor_copy, w30_raw[:], "w30_bf")
-        w11_bf = round_weight(nc.vector.tensor_copy, w11_raw[:], "w11_bf")
+        round_into(nc.vector.tensor_copy, late_bf[:, : 4 * P], w11_raw[:])
         w30_q = quantize(w30_bf, (P,), "w30")
-        w11_q = quantize(w11_bf, (P,), "w11")
-        w31_bf = round_weight(round_on_gpsimd, w31_raw[:], "w31_bf", "w11_bf")
+        late_q = quantize(late_bf, (N,), "late")
+        w31_bf = round_weight(round_on_gpsimd, w31_raw[:], "w31_bf", "late_bf")
+
+        def block_of(quantized, block=0):
+            return [part[:, block * P : (block + 1) * P] for part in quantized]
 
         def product(w_q, rows, c0, c1, number, copy):
             half = c0 // HALF
@@ -155,8 +159,8 @@ def tile_picked_gatedg_relu_e_kernel(tc, xT, w1, w2, w3, offs, cen, pos1, pos2, 
             nodes = slice(c0 - half * HALF, c1 - half * HALF)
             nc.tensor.matmul_mx(
                 out=acc[:],
-                lhsT=w_q[0][:].bitcast(FP8X4),
-                lhsT_scale=w_q[1][:],
+                lhsT=w_q[0].bitcast(FP8X4),
+                lhsT_scale=w_q[1],
                 rhs=x_q[half][0][:, nodes].bitcast(FP8X4),
                 rhs_scale=x_q[half][1][:, nodes],
                 start=True,
@@ -211,12 +215,11 @@ def tile_picked_gatedg_relu_e_kernel(tc, xT, w1, w2, w3, offs, cen, pos1, pos2, 
         yc0 = sbuf(V, F32, "yc0")
         cuts = (0, QUARTER, HALF, HALF + QUARTER, S - P, S)
         for i in range(5):
-            product(w10_q, y0, cuts[i], cuts[i + 1], i, nc.scalar.copy)
+            product(block_of(w10_q), y0, cuts[i], cuts[i + 1], i, nc.scalar.copy)
         for q in range(4):
-            product(w20_q, e0, q * QUARTER, (q + 1) * QUARTER, (5 + q) % 8, nc.vector.tensor_copy if q > 0 else nc.scalar.copy)
+            product(block_of(w20_q), e0, q * QUARTER, (q + 1) * QUARTER, (5 + q) % 8, nc.vector.tensor_copy if q > 0 else nc.scalar.copy)
             if q == 0:
                 centres(yc0, y0, 0, V)
-        w21_q = quantize(w21_bf, (P,), "w21", "w20_codes")
         w31_q = quantize(w31_bf, (P,), "w31")
 
         pre00 = sbuf(V, F32, "pre00")
@@ -226,15 +229,15 @@ def tile_picked_gatedg_relu_e_kernel(tc, xT, w1, w2, w3, offs, cen, pos1, pos2, 
 
         h0 = sbuf(S, F32, "h0")
         for q in range(4):
-            product(w30_q, h0, q * QUARTER, (q + 1) * QUARTER, 1 + q, nc.scalar.copy)
+            product(block_of(w30_q), h0, q * QUARTER, (q + 1) * QUARTER, 1 + q, nc.scalar.copy)
         y1 = sbuf(S, F32, "y1")
-        product(w11_q, y1, 0, HALF, 5, nc.scalar.copy)
+        product(block_of(late_q, 0), y1, 0, HALF, 5, nc.scalar.copy)
         gate00 = sigmoid(pre00, "gate00")
-        product(w11_q, y1, HALF, S, 6, nc.scalar.copy)
+        product(block_of(late_q, 0), y1, HALF, S, 6, nc.scalar.copy)
         e1 = sbuf(S, F32, "e1")
-        product(w21_q, e1, 0, HALF, 5, nc.scalar.copy)
+        product(block_of(late_q, 1), e1, 0, HALF, 5, nc.scalar.copy)
         gate01 = sigmoid(pre01, "gate01")
-        product(w21_q, e1, HALF, S, 6, nc.scalar.copy)
+        product(block_of(late_q, 1), e1, HALF, S, 6, nc.scalar.copy)
         msg00 = sbuf(V, F32, "msg00")
         msg01 = sbuf(V, F32, "msg01")
         neighbours(msg00[:], h0, 0, 0, V, gate00[:], ALU.mult)
@@ -248,7 +251,7 @@ def tile_picked_gatedg_relu_e_kernel(tc, xT, w1, w2, w3, offs, cen, pos1, pos2, 
             centres(yc1, y1, c0, c1)
             neighbours(pre10[:, c0:c1], e1, 0, c0, c1, yc1[:, c0:c1], ALU.add)
         neighbours(pre11[:], e1, 1, 0, V, yc1[:], ALU.add)
-        h1 = product_in_halves(w31_q, "h1", (5, 6))
+        h1 = product_in_halves(block_of(w31_q), "h1", (5, 6))
         gate10 = sigmoid(pre10, "gate10")
         fetched = sbuf(SIDE, F32, "fetched")
         nc.scalar.activation(fetched[:], h1[:].indirect(entries(pos_t[1], SIDE, V)), ACT.Copy)

@@ -69,8 +69,12 @@ def tile_picked_gatedg_relu_e_kernel(tc, xT, w1, w2, w3, offs, cen, pos1, pos2, 
             round_into(copy, grouped[:], raw)
             return grouped
 
-        def round_on_gpsimd(dst, src):
-            nc.gpsimd.tensor_scalar(dst, src, 1.0, 0.0, ALU.mult, ALU.add)
+        def round_on_gpsimd(raw, name, tag=None):
+            grouped = sbuf(4 * raw.shape[2], BF16, name, tag)
+            nc.gpsimd.tensor_scalar(
+                grouped[:].rearrange("p (n j) -> p n j", j=4), raw.rearrange("p j n -> p n j"), 1.0, 0.0, ALU.mult, ALU.add
+            )
+            return grouped
 
         def quantize(grouped, widths, name, tag=None):
             codes = sbuf(sum(widths), U32, name + "_codes", tag)
@@ -134,7 +138,7 @@ def tile_picked_gatedg_relu_e_kernel(tc, xT, w1, w2, w3, offs, cen, pos1, pos2, 
                 round_plane(j)
             gather_plane(j)
 
-        w10_bf = round_weight(round_on_gpsimd, w10_raw[:], "w10_bf")
+        w10_bf = round_on_gpsimd(w10_raw[:], "w10_bf")
         w20_bf = round_weight(nc.scalar.copy, w2_raw[:, :, 0:P], "w20_bf")
         w10_q = quantize(w10_bf, (P,), "w10")
         x_q = [
@@ -148,7 +152,7 @@ def tile_picked_gatedg_relu_e_kernel(tc, xT, w1, w2, w3, offs, cen, pos1, pos2, 
         round_into(nc.vector.tensor_copy, late_bf[:, : 4 * P], w11_raw[:])
         w30_q = quantize(w30_bf, (P,), "w30")
         late_q = quantize(late_bf, (N,), "late")
-        w31_bf = round_weight(round_on_gpsimd, w31_raw[:], "w31_bf", "late_bf")
+        w31_bf = round_on_gpsimd(w31_raw[:], "w31_bf", "late_bf")
 
         def block_of(quantized, block=0):
             return [part[:, block * P : (block + 1) * P] for part in quantized]

@@ -24,8 +24,7 @@ RUN = 4
 ALIGN = 256
 
 LOADS = ((4096,), (4096,), (2048, 2048), (2048, 1536, 512))
-SHARED = (2, 3)
-SCALAR_COLUMNS = 512
+SCALAR_COLUMNS = {2: (1536, 512), 3: (0, 512, 256)}
 
 
 def tile_picked_gatedg_relu_e_kernel(tc, xT, w1, w2, w3, offs, cen, pos1, pos2, out):
@@ -91,7 +90,7 @@ def tile_picked_gatedg_relu_e_kernel(tc, xT, w1, w2, w3, offs, cen, pos1, pos2, 
 
         x_rows = xT.rearrange("(p j) t -> p j t", j=4)
         planes = [sbuf(T, F32, "plane%d" % j) for j in range(4)]
-        rounded = {j: sbuf(T, BF16, "rounded%d" % j) for j in SHARED}
+        rounded = {j: sbuf(T, BF16, "rounded%d" % j) for j in SCALAR_COLUMNS}
         x_first = sbuf(4 * HALF, BF16, "x_first")
         x_second = sbuf(4 * HALF, BF16, "x_second")
 
@@ -106,17 +105,19 @@ def tile_picked_gatedg_relu_e_kernel(tc, xT, w1, w2, w3, offs, cen, pos1, pos2, 
 
         def round_plane(j):
             c0 = 0
-            for width in LOADS[j]:
-                cut = c0 + width - min(SCALAR_COLUMNS, width // 2)
-                nc.vector.tensor_copy(rounded[j][:, c0:cut], planes[j][:, c0:cut])
-                nc.scalar.copy(rounded[j][:, cut : c0 + width], planes[j][:, cut : c0 + width])
+            for width, share in zip(LOADS[j], SCALAR_COLUMNS[j]):
+                cut = c0 + width - share
+                if share < width:
+                    nc.vector.tensor_copy(rounded[j][:, c0:cut], planes[j][:, c0:cut])
+                if share > 0:
+                    nc.scalar.copy(rounded[j][:, cut : c0 + width], planes[j][:, cut : c0 + width])
                 c0 = c0 + width
 
         def gather_plane(j):
             first = x_first[:].rearrange("p (n j) -> p n j", j=4)[:, :, j]
             second = x_second[:].rearrange("p (n j) -> p n j", j=4)[:, :, j]
             nc.vector.tensor_copy(first, planes[j][:].indirect(entries(offs_t, 0, HALF)))
-            if j in SHARED:
+            if j in SCALAR_COLUMNS:
                 nc.scalar.activation(second, rounded[j][:].indirect(entries(offs_t, HALF, S)), ACT.Copy)
             else:
                 nc.vector.tensor_copy(second, planes[j][:].indirect(entries(offs_t, HALF, S)))
@@ -134,7 +135,7 @@ def tile_picked_gatedg_relu_e_kernel(tc, xT, w1, w2, w3, offs, cen, pos1, pos2, 
         pos_t = [load_list(pos1, "pos1_t"), load_list(pos2, "pos2_t")]
 
         for j in range(4):
-            if j in SHARED:
+            if j in SCALAR_COLUMNS:
                 round_plane(j)
             gather_plane(j)
 

@@ -23,9 +23,6 @@ PER_COLUMN = 16
 RUN = 4
 ALIGN = 256
 
-LOADS = ((4096,), (4096,), (2048, 2048), (2048, 1536, 512))
-SCALAR_COLUMNS = {2: (1536, 512), 3: (0, 512, 256)}
-
 
 def tile_picked_gatedg_relu_e_kernel(tc, xT, w1, w2, w3, offs, cen, pos1, pos2, out):
     nc = tc.nc
@@ -90,37 +87,23 @@ def tile_picked_gatedg_relu_e_kernel(tc, xT, w1, w2, w3, offs, cen, pos1, pos2, 
 
         x_rows = xT.rearrange("(p j) t -> p j t", j=4)
         planes = [sbuf(T, F32, "plane%d" % j) for j in range(4)]
-        rounded = {j: sbuf(T, BF16, "rounded%d" % j) for j in SCALAR_COLUMNS}
-        x_first = sbuf(4 * HALF, BF16, "x_first")
-        x_second = sbuf(4 * HALF, BF16, "x_second")
+        x_vector = sbuf(4 * HALF, BF16, "x_vector")
+        x_scalar = [sbuf(4 * QUARTER, BF16, "x_scalar%d" % i) for i in range(2)]
 
         def entries(lst, c0, c1):
             return lst[:, c0 // PER_COLUMN : c1 // PER_COLUMN]
 
         def load_plane(j):
-            c0 = 0
-            for width in LOADS[j]:
-                nc.sync.dma_start(planes[j][:, c0 : c0 + width], x_rows[:, j, c0 : c0 + width])
-                c0 = c0 + width
+            nc.sync.dma_start(planes[j][:], x_rows[:, j, :])
 
-        def round_plane(j):
-            c0 = 0
-            for width, share in zip(LOADS[j], SCALAR_COLUMNS[j]):
-                cut = c0 + width - share
-                if share < width:
-                    nc.vector.tensor_copy(rounded[j][:, c0:cut], planes[j][:, c0:cut])
-                if share > 0:
-                    nc.scalar.copy(rounded[j][:, cut : c0 + width], planes[j][:, cut : c0 + width])
-                c0 = c0 + width
+        def slot(grouped, j):
+            return grouped[:].rearrange("p (n j) -> p n j", j=4)[:, :, j]
 
         def gather_plane(j):
-            first = x_first[:].rearrange("p (n j) -> p n j", j=4)[:, :, j]
-            second = x_second[:].rearrange("p (n j) -> p n j", j=4)[:, :, j]
-            nc.vector.tensor_copy(first, planes[j][:].indirect(entries(offs_t, 0, HALF)))
-            if j in SCALAR_COLUMNS:
-                nc.scalar.activation(second, rounded[j][:].indirect(entries(offs_t, HALF, S)), ACT.Copy)
-            else:
-                nc.vector.tensor_copy(second, planes[j][:].indirect(entries(offs_t, HALF, S)))
+            nc.vector.tensor_copy(slot(x_vector, j), planes[j][:].indirect(entries(offs_t, 0, HALF)))
+            for i in range(2):
+                c0 = HALF + i * QUARTER
+                nc.scalar.activation(slot(x_scalar[i], j), planes[j][:].indirect(entries(offs_t, c0, c0 + QUARTER)), ACT.Copy)
 
         load_plane(0)
         offs_t = load_list(offs, "offs_t")
@@ -135,17 +118,26 @@ def tile_picked_gatedg_relu_e_kernel(tc, xT, w1, w2, w3, offs, cen, pos1, pos2, 
         pos_t = [load_list(pos1, "pos1_t"), load_list(pos2, "pos2_t")]
 
         for j in range(4):
-            if j in SCALAR_COLUMNS:
-                round_plane(j)
             gather_plane(j)
 
         w10_bf = round_on_gpsimd(w10_raw[:], "w10_bf")
         w20_bf = round_weight(nc.scalar.copy, w2_raw[:, :, 0:P], "w20_bf")
         w10_q = quantize(w10_bf, (P,), "w10")
-        x_q = [
-            quantize(x_first, (QUARTER, QUARTER), "x_first", "w10_raw"),
-            quantize(x_second, (QUARTER, P, P), "x_second"),
-        ]
+        x_codes = sbuf(S, U32, "x_codes", "w10_raw")
+        x_scales = sbuf(S, U8, "x_scales")
+        pieces = (
+            (x_scalar[0], HALF, HALF, HALF + QUARTER),
+            (x_vector, 0, 0, QUARTER),
+            (x_vector, 0, QUARTER, HALF),
+            (x_scalar[1], HALF + QUARTER, HALF + QUARTER, S - P),
+            (x_scalar[1], HALF + QUARTER, S - P, S),
+        )
+        for grouped, base, c0, c1 in pieces:
+            nc.vector.quantize_mx(
+                out=x_codes[:, c0:c1].bitcast(FP8X4),
+                scales=x_scales[:, c0:c1],
+                in_=grouped[:, 4 * (c0 - base) : 4 * (c1 - base)],
+            )
         w20_q = quantize(w20_bf, (P,), "w20")
         late_bf = sbuf(4 * N, BF16, "late_bf")
         round_into(nc.vector.tensor_copy, late_bf[:, 4 * P :], w2_raw[:, :, P:N])
@@ -159,15 +151,13 @@ def tile_picked_gatedg_relu_e_kernel(tc, xT, w1, w2, w3, offs, cen, pos1, pos2, 
             return [part[:, block * P : (block + 1) * P] for part in quantized]
 
         def product(w_q, rows, c0, c1, number, copy):
-            half = c0 // HALF
             acc = bank(number, c1 - c0)
-            nodes = slice(c0 - half * HALF, c1 - half * HALF)
             nc.tensor.matmul_mx(
                 out=acc[:],
                 lhsT=w_q[0].bitcast(FP8X4),
                 lhsT_scale=w_q[1],
-                rhs=x_q[half][0][:, nodes].bitcast(FP8X4),
-                rhs_scale=x_q[half][1][:, nodes],
+                rhs=x_codes[:, c0:c1].bitcast(FP8X4),
+                rhs_scale=x_scales[:, c0:c1],
                 start=True,
                 stop=True,
             )
@@ -218,9 +208,8 @@ def tile_picked_gatedg_relu_e_kernel(tc, xT, w1, w2, w3, offs, cen, pos1, pos2, 
         y0 = sbuf(S, F32, "y0")
         e0 = sbuf(S, F32, "e0")
         yc0 = sbuf(V, F32, "yc0")
-        cuts = (0, QUARTER, HALF, HALF + QUARTER, S - P, S)
-        for i in range(5):
-            product(block_of(w10_q), y0, cuts[i], cuts[i + 1], i, nc.scalar.copy)
+        for i, piece in enumerate(pieces):
+            product(block_of(w10_q), y0, piece[2], piece[3], i, nc.scalar.copy)
         for q in range(4):
             product(block_of(w20_q), e0, q * QUARTER, (q + 1) * QUARTER, (5 + q) % 8, nc.vector.tensor_copy if q > 0 else nc.scalar.copy)
             if q == 0:

@@ -145,7 +145,6 @@ def tile_picked_gatedg_relu_e_kernel(tc, xT, w1, w2, w3, offs, cen, pos1, pos2, 
         round_into(nc.vector.tensor_copy, late_bf[:, : 4 * P], w11_raw[:])
         w30_q = quantize(w30_bf, (P,), "w30")
         late_q = quantize(late_bf, (N,), "late")
-        w31_bf = round_on_gpsimd(w31_raw[:], "w31_bf", "late_bf")
 
         def block_of(quantized, block=0):
             return [part[:, block * P : (block + 1) * P] for part in quantized]
@@ -214,11 +213,12 @@ def tile_picked_gatedg_relu_e_kernel(tc, xT, w1, w2, w3, offs, cen, pos1, pos2, 
             product(block_of(w20_q), e0, q * QUARTER, (q + 1) * QUARTER, (5 + q) % 8, nc.vector.tensor_copy if q > 0 else nc.scalar.copy)
             if q == 0:
                 centres(yc0, y0, 0, V)
-        w31_q = quantize(w31_bf, (P,), "w31")
+        w31_bf = round_weight(nc.vector.tensor_copy, w31_raw[:], "w31_bf")
 
         pre00 = sbuf(V, F32, "pre00")
         pre01 = sbuf(V, F32, "pre01")
         neighbours(pre00[:], e0, 0, 0, V, yc0[:], ALU.add)
+        w31_q = quantize(w31_bf, (P,), "w31")
         neighbours(pre01[:], e0, 1, 0, V, yc0[:], ALU.add)
 
         h0 = sbuf(S, F32, "h0")

@@ -229,9 +229,9 @@ def tile_picked_gatedg_relu_e_kernel(tc, xT, w1, w2, w3, offs, cen, pos1, pos2, 
         gate00 = sigmoid(pre00, "gate00")
         product(block_of(late_q, 0), y1, HALF, S, 6, nc.scalar.copy)
         e1 = sbuf(S, F32, "e1")
-        product(block_of(late_q, 1), e1, 0, HALF, 5, nc.scalar.copy)
+        product(block_of(late_q, 1), e1, 0, HALF, 7, nc.scalar.copy)
         gate01 = sigmoid(pre01, "gate01")
-        product(block_of(late_q, 1), e1, HALF, S, 6, nc.scalar.copy)
+        product(block_of(late_q, 1), e1, HALF, S, 5, nc.scalar.copy)
         msg00 = sbuf(V, F32, "msg00")
         msg01 = sbuf(V, F32, "msg01")
         neighbours(msg00[:], h0, 0, 0, V, gate00[:], ALU.mult)
@@ -245,13 +245,13 @@ def tile_picked_gatedg_relu_e_kernel(tc, xT, w1, w2, w3, offs, cen, pos1, pos2, 
             centres(yc1, y1, c0, c1)
             neighbours(pre10[:, c0:c1], e1, 0, c0, c1, yc1[:, c0:c1], ALU.add)
         neighbours(pre11[:], e1, 1, 0, V, yc1[:], ALU.add)
-        h1 = product_in_halves(block_of(w31_q), "h1", (5, 6))
+        h1 = product_in_halves(block_of(w31_q), "h1", (6, 7))
         gate10 = sigmoid(pre10, "gate10")
-        fetched = sbuf(SIDE, F32, "fetched")
-        nc.scalar.activation(fetched[:], h1[:].indirect(entries(pos_t[1], SIDE, V)), ACT.Copy)
-        gate11 = sigmoid(pre11, "gate11")
         turned = [sum_turned([msg00[:, c0:c1], msg01[:, c0:c1]], 5 + i) for i, (c0, c1) in enumerate(sides)]
         relus = [relu_turned(part, "relu%d" % i) for i, part in enumerate(turned)]
+        gate11 = sigmoid(pre11, "gate11")
+        fetched = sbuf(SIDE, F32, "fetched")
+        nc.scalar.activation(fetched[:], h1[:].indirect(entries(pos_t[1], SIDE, V)), ACT.Copy)
         for i, (c0, c1) in enumerate(sides):
             turn_back_and_store(relus[i], 1 + i, 0, c0, "res0_%d" % i)
 
@@ -262,7 +262,7 @@ def tile_picked_gatedg_relu_e_kernel(tc, xT, w1, w2, w3, offs, cen, pos1, pos2, 
         nc.vector.tensor_tensor(msg11[:, SIDE:], fetched[:], gate11[:, SIDE:], ALU.mult)
         totals = []
         for i, (c0, c1) in enumerate(sides):
-            total = sbuf(SIDE, F32, "total%d" % i)
+            total = sbuf(SIDE, F32, "total%d" % i, ("h1", "total1")[i])
             nc.vector.tensor_tensor(total[:], msg10[:, c0:c1], msg11[:, c0:c1], ALU.add)
             totals.append(total)
         for i, (c0, c1) in enumerate(sides):

@@ -110,18 +110,18 @@ def tile_picked_gatedg_relu_e_kernel(tc, xT, w1, w2, w3, offs, cen, pos1, pos2, 
         for j in range(1, 4):
             load_plane(j)
         w10_raw = load_weight(w1, 0, P, "w10_raw")
-        w2_raw = load_weight(w2, 0, N, "w2_raw")
-        w30_raw = load_weight(w3, 0, P, "w30_raw")
+        w20_raw = load_weight(w2, 0, P, "w20_raw")
+        w3_raw = load_weight(w3, 0, N, "w3_raw")
         w11_raw = load_weight(w1, P, N, "w11_raw")
         cen_t = load_list(cen, "cen_t")
-        w31_raw = load_weight(w3, P, N, "w31_raw")
+        w21_raw = load_weight(w2, P, N, "w21_raw")
         pos_t = [load_list(pos1, "pos1_t"), load_list(pos2, "pos2_t")]
 
         for j in range(4):
             gather_plane(j)
 
         w10_bf = round_on_gpsimd(w10_raw[:], "w10_bf")
-        w20_bf = round_weight(nc.scalar.copy, w2_raw[:, :, 0:P], "w20_bf")
+        w20_bf = round_weight(nc.scalar.copy, w20_raw[:], "w20_bf")
         w10_q = quantize(w10_bf, (P,), "w10")
         x_codes = sbuf(S, U32, "x_codes", "w10_raw")
         x_scales = sbuf(S, U8, "x_scales")
@@ -139,12 +139,10 @@ def tile_picked_gatedg_relu_e_kernel(tc, xT, w1, w2, w3, offs, cen, pos1, pos2, 
                 in_=grouped[:, 4 * (c0 - base) : 4 * (c1 - base)],
             )
         w20_q = quantize(w20_bf, (P,), "w20")
-        late_bf = sbuf(4 * N, BF16, "late_bf")
-        round_into(nc.vector.tensor_copy, late_bf[:, 4 * P :], w2_raw[:, :, P:N])
-        w30_bf = round_weight(nc.vector.tensor_copy, w30_raw[:], "w30_bf")
-        round_into(nc.vector.tensor_copy, late_bf[:, : 4 * P], w11_raw[:])
-        w30_q = quantize(w30_bf, (P,), "w30")
-        late_q = quantize(late_bf, (N,), "late")
+        w3_bf = round_weight(nc.vector.tensor_copy, w3_raw[:], "w3_bf")
+        w11_bf = round_weight(nc.vector.tensor_copy, w11_raw[:], "w11_bf")
+        w3_q = quantize(w3_bf, (N,), "w3")
+        w11_q = quantize(w11_bf, (P,), "w11")
 
         def block_of(quantized, block=0):
             return [part[:, block * P : (block + 1) * P] for part in quantized]
@@ -213,25 +211,25 @@ def tile_picked_gatedg_relu_e_kernel(tc, xT, w1, w2, w3, offs, cen, pos1, pos2, 
             product(block_of(w20_q), e0, q * QUARTER, (q + 1) * QUARTER, (5 + q) % 8, nc.vector.tensor_copy if q > 0 else nc.scalar.copy)
             if q == 0:
                 centres(yc0, y0, 0, V)
-        w31_bf = round_weight(nc.vector.tensor_copy, w31_raw[:], "w31_bf")
+        w21_bf = round_weight(nc.vector.tensor_copy, w21_raw[:], "w21_bf")
 
         pre00 = sbuf(V, F32, "pre00")
         pre01 = sbuf(V, F32, "pre01")
         neighbours(pre00[:], e0, 0, 0, V, yc0[:], ALU.add)
-        w31_q = quantize(w31_bf, (P,), "w31")
+        w21_q = quantize(w21_bf, (P,), "w21")
         neighbours(pre01[:], e0, 1, 0, V, yc0[:], ALU.add)
 
         h0 = sbuf(S, F32, "h0")
         for q in range(4):
-            product(block_of(w30_q), h0, q * QUARTER, (q + 1) * QUARTER, 1 + q, nc.scalar.copy)
+            product(block_of(w3_q, 0), h0, q * QUARTER, (q + 1) * QUARTER, 1 + q, nc.scalar.copy)
         y1 = sbuf(S, F32, "y1")
-        product(block_of(late_q, 0), y1, 0, HALF, 5, nc.scalar.copy)
+        product(block_of(w11_q), y1, 0, HALF, 5, nc.scalar.copy)
         gate00 = sigmoid(pre00, "gate00")
-        product(block_of(late_q, 0), y1, HALF, S, 6, nc.scalar.copy)
+        product(block_of(w11_q), y1, HALF, S, 6, nc.scalar.copy)
         e1 = sbuf(S, F32, "e1")
-        product(block_of(late_q, 1), e1, 0, HALF, 7, nc.scalar.copy)
+        product(block_of(w21_q), e1, 0, HALF, 7, nc.scalar.copy)
         gate01 = sigmoid(pre01, "gate01")
-        product(block_of(late_q, 1), e1, HALF, S, 5, nc.scalar.copy)
+        product(block_of(w21_q), e1, HALF, S, 5, nc.scalar.copy)
         msg00 = sbuf(V, F32, "msg00")
         msg01 = sbuf(V, F32, "msg01")
         neighbours(msg00[:], h0, 0, 0, V, gate00[:], ALU.mult)
@@ -245,7 +243,7 @@ def tile_picked_gatedg_relu_e_kernel(tc, xT, w1, w2, w3, offs, cen, pos1, pos2, 
             centres(yc1, y1, c0, c1)
             neighbours(pre10[:, c0:c1], e1, 0, c0, c1, yc1[:, c0:c1], ALU.add)
         neighbours(pre11[:], e1, 1, 0, V, yc1[:], ALU.add)
-        h1 = product_in_halves(block_of(w31_q), "h1", (6, 7))
+        h1 = product_in_halves(block_of(w3_q, 1), "h1", (6, 7))
         gate10 = sigmoid(pre10, "gate10")
         turned = [sum_turned([msg00[:, c0:c1], msg01[:, c0:c1]], 5 + i) for i, (c0, c1) in enumerate(sides)]
         relus = [relu_turned(part, "relu%d" % i) for i, part in enumerate(turned)]

@@ -111,8 +111,8 @@ def tile_picked_gatedg_relu_e_kernel(tc, xT, w1, w2, w3, offs, cen, pos1, pos2, 
             load_plane(j)
         w10_raw = load_weight(w1, 0, P, "w10_raw")
         w20_raw = load_weight(w2, 0, P, "w20_raw")
-        w3_raw = load_weight(w3, 0, N, "w3_raw")
         w11_raw = load_weight(w1, P, N, "w11_raw")
+        w3_raw = load_weight(w3, 0, N, "w3_raw")
         cen_t = load_list(cen, "cen_t")
         w21_raw = load_weight(w2, P, N, "w21_raw")
         pos_t = [load_list(pos1, "pos1_t"), load_list(pos2, "pos2_t")]
@@ -122,6 +122,8 @@ def tile_picked_gatedg_relu_e_kernel(tc, xT, w1, w2, w3, offs, cen, pos1, pos2, 
 
         w10_bf = round_on_gpsimd(w10_raw[:], "w10_bf")
         w20_bf = round_weight(nc.scalar.copy, w20_raw[:], "w20_bf")
+        w11_bf = sbuf(4 * P, BF16, "w11_bf")
+        round_into(nc.scalar.copy, w11_bf[:, : 2 * P], w11_raw[:, :, : P // 2])
         w10_q = quantize(w10_bf, (P,), "w10")
         x_codes = sbuf(S, U32, "x_codes", "w10_raw")
         x_scales = sbuf(S, U8, "x_scales")
@@ -139,10 +141,10 @@ def tile_picked_gatedg_relu_e_kernel(tc, xT, w1, w2, w3, offs, cen, pos1, pos2, 
                 in_=grouped[:, 4 * (c0 - base) : 4 * (c1 - base)],
             )
         w20_q = quantize(w20_bf, (P,), "w20")
+        round_into(nc.vector.tensor_copy, w11_bf[:, 2 * P :], w11_raw[:, :, P // 2 :])
         w3_bf = round_weight(nc.vector.tensor_copy, w3_raw[:], "w3_bf")
-        w11_bf = round_weight(nc.vector.tensor_copy, w11_raw[:], "w11_bf")
-        w3_q = quantize(w3_bf, (N,), "w3")
         w11_q = quantize(w11_bf, (P,), "w11")
+        w3_q = quantize(w3_bf, (N,), "w3")
 
         def block_of(quantized, block=0):
             return [part[:, block * P : (block + 1) * P] for part in quantized]

@@ -213,6 +213,8 @@ def tile_picked_gatedg_relu_e_kernel(tc, xT, w1, w2, w3, offs, cen, pos1, pos2, 
             product(block_of(w20_q), e0, q * QUARTER, (q + 1) * QUARTER, (5 + q) % 8, nc.vector.tensor_copy if q > 0 else nc.scalar.copy)
             if q == 0:
                 centres(yc0, y0, 0, V)
+        h0 = sbuf(S, F32, "h0")
+        product(block_of(w3_q, 0), h0, 0, P, 1, nc.vector.tensor_copy)
         w21_bf = round_weight(nc.vector.tensor_copy, w21_raw[:], "w21_bf")
 
         pre00 = sbuf(V, F32, "pre00")
@@ -221,9 +223,8 @@ def tile_picked_gatedg_relu_e_kernel(tc, xT, w1, w2, w3, offs, cen, pos1, pos2, 
         w21_q = quantize(w21_bf, (P,), "w21")
         neighbours(pre01[:], e0, 1, 0, V, yc0[:], ALU.add)
 
-        h0 = sbuf(S, F32, "h0")
-        for q in range(4):
-            product(block_of(w3_q, 0), h0, q * QUARTER, (q + 1) * QUARTER, 1 + q, nc.scalar.copy)
+        for number, c0, c1 in ((2, P, QUARTER), (3, QUARTER, HALF), (4, HALF, S)):
+            product(block_of(w3_q, 0), h0, c0, c1, number, nc.scalar.copy)
         y1 = sbuf(S, F32, "y1")
         product(block_of(w11_q), y1, 0, HALF, 5, nc.scalar.copy)
         gate00 = sigmoid(pre00, "gate00")

from contextlib import ExitStack

import concourse.mybir as mybir
from concourse.masks import make_identity

K, T, S, V, N = 512, 4096, 1024, 512, 256
FLOPS = 3 * 2 * K * N * S

F32 = mybir.dt.float32
BF16 = mybir.dt.bfloat16
U32 = mybir.dt.uint32
U16 = mybir.dt.uint16
U8 = mybir.dt.uint8
FP8X4 = mybir.dt.float8_e4m3fn_x4
ACT = mybir.ActivationFunctionType
ALU = mybir.AluOpType

P = 128
HALF = S // 2
QUARTER = S // 4
SIDE = V // 2
PER_COLUMN = 16
RUN = 4
ALIGN = 256


def tile_picked_gatedg_relu_e_kernel(tc, xT, w1, w2, w3, offs, cen, pos1, pos2, out):
    nc = tc.nc
    with ExitStack() as ctx:
        keep = ctx.enter_context(tc.tile_pool(name="keep", bufs=1))
        psum = ctx.enter_context(tc.psum_pool(name="psum", bufs=1))

        def sbuf(width, dtype, name, tag=None):
            return keep.tile([P, width], dtype, name=name, tag=tag or name, align_bytes=ALIGN)

        def bank(number, width):
            return psum.tile([P, width], F32, name="bank", tag="bank%d" % number)

        warm_in = keep.tile([P, 8], F32, name="warm_in")
        warm_out = keep.tile([P, 8], F32, name="warm_out")
        nc.vector.memset(warm_in[:], 0.0)
        nc.scalar.activation(warm_out[:], warm_in[:], ACT.Sigmoid)

        identity = sbuf(P, F32, "identity")
        make_identity(nc, identity[:])

        def load_list(src, name):
            entries = keep.tile(list(src.shape), U16, name=name)
            nc.sync.dma_start(entries[:], src)
            return entries

        def load_weight(w, c0, c1, name):
            raw = keep.tile([P, 4, c1 - c0], F32, name=name, tag=name, align_bytes=ALIGN)
            nc.sync.dma_start(raw[:], w.rearrange("(p j) n -> p j n", j=4)[:, :, c0:c1])
            return raw

        def round_into(copy, grouped, raw):
            copy(
                grouped.rearrange("p (c i j) -> p c j i", i=RUN, j=4),
                raw.rearrange("p j (c i) -> p c j i", i=RUN),
            )

        def round_weight(copy, raw, name, tag=None):
            grouped = sbuf(4 * raw.shape[2], BF16, name, tag)
            round_into(copy, grouped[:], raw)
            return grouped

        def round_on_gpsimd(raw, name, tag=None):
            grouped = sbuf(4 * raw.shape[2], BF16, name, tag)
            nc.gpsimd.tensor_scalar(
                grouped[:].rearrange("p (n j) -> p n j", j=4), raw.rearrange("p j n -> p n j"), 1.0, 0.0, ALU.mult, ALU.add
            )
            return grouped

        def quantize(grouped, widths, name, tag=None):
            codes = sbuf(sum(widths), U32, name + "_codes", tag)
            scales = sbuf(sum(widths), U8, name + "_scales")
            c0 = 0
            for width in widths:
                nc.vector.quantize_mx(
                    out=codes[:, c0 : c0 + width].bitcast(FP8X4),
                    scales=scales[:, c0 : c0 + width],
                    in_=grouped[:, 4 * c0 : 4 * (c0 + width)],
                )
                c0 = c0 + width
            return codes, scales

        x_rows = xT.rearrange("(p j) t -> p j t", j=4)
        planes = [sbuf(T, F32, "plane%d" % j) for j in range(4)]
        x_vector = sbuf(4 * HALF, BF16, "x_vector")
        x_scalar = [sbuf(4 * QUARTER, BF16, "x_scalar%d" % i) for i in range(2)]

        def entries(lst, c0, c1):
            return lst[:, c0 // PER_COLUMN : c1 // PER_COLUMN]

        def load_plane(j):
            nc.sync.dma_start(planes[j][:], x_rows[:, j, :])

        def slot(grouped, j):
            return grouped[:].rearrange("p (n j) -> p n j", j=4)[:, :, j]

        def gather_plane(j):
            nc.vector.tensor_copy(slot(x_vector, j), planes[j][:].indirect(entries(offs_t, 0, HALF)))
            for i in range(2):
                c0 = HALF + i * QUARTER
                nc.scalar.activation(slot(x_scalar[i], j), planes[j][:].indirect(entries(offs_t, c0, c0 + QUARTER)), ACT.Copy)

        load_plane(0)
        offs_t = load_list(offs, "offs_t")
        for j in range(1, 4):
            load_plane(j)
        w10_raw = load_weight(w1, 0, P, "w10_raw")
        w20_raw = load_weight(w2, 0, P, "w20_raw")
        w11_raw = load_weight(w1, P, N, "w11_raw")
        w3_raw = load_weight(w3, 0, N, "w3_raw")
        cen_t = load_list(cen, "cen_t")
        w21_raw = load_weight(w2, P, N, "w21_raw")
        pos_t = [load_list(pos1, "pos1_t"), load_list(pos2, "pos2_t")]

        for j in range(4):
            gather_plane(j)

        w10_bf = round_on_gpsimd(w10_raw[:], "w10_bf")
        w20_bf = round_weight(nc.scalar.copy, w20_raw[:], "w20_bf")
        w11_bf = sbuf(4 * P, BF16, "w11_bf")
        round_into(nc.scalar.copy, w11_bf[:, : 2 * P], w11_raw[:, :, : P // 2])
        w10_q = quantize(w10_bf, (P,), "w10")
        x_codes = sbuf(S, U32, "x_codes", "w10_raw")
        x_scales = sbuf(S, U8, "x_scales")
        pieces = (
            (x_scalar[0], HALF, HALF, HALF + QUARTER),
            (x_vector, 0, 0, QUARTER),
            (x_vector, 0, QUARTER, HALF),
            (x_scalar[1], HALF + QUARTER, HALF + QUARTER, S - P),
            (x_scalar[1], HALF + QUARTER, S - P, S),
        )
        for grouped, base, c0, c1 in pieces:
            nc.vector.quantize_mx(
                out=x_codes[:, c0:c1].bitcast(FP8X4),
                scales=x_scales[:, c0:c1],
                in_=grouped[:, 4 * (c0 - base) : 4 * (c1 - base)],
            )
        w20_q = quantize(w20_bf, (P,), "w20")
        round_into(nc.vector.tensor_copy, w11_bf[:, 2 * P :], w11_raw[:, :, P // 2 :])
        w3_bf = round_weight(nc.vector.tensor_copy, w3_raw[:], "w3_bf")
        w11_q = quantize(w11_bf, (P,), "w11")
        w3_q = quantize(w3_bf, (N,), "w3")

        def block_of(quantized, block=0):
            return [part[:, block * P : (block + 1) * P] for part in quantized]

        def product(w_q, rows, c0, c1, number, copy):
            acc = bank(number, c1 - c0)
            nc.tensor.matmul_mx(
                out=acc[:],
                lhsT=w_q[0].bitcast(FP8X4),
                lhsT_scale=w_q[1],
                rhs=x_codes[:, c0:c1].bitcast(FP8X4),
                rhs_scale=x_scales[:, c0:c1],
                start=True,
                stop=True,
            )
            copy(rows[:, c0:c1], acc[:])

        def product_in_halves(w_q, name, banks):
            rows = sbuf(S, F32, name)
            for half in range(2):
                product(w_q, rows, half * HALF, (half + 1) * HALF, banks[half], nc.scalar.copy)
            return rows

        def centres(yc, y, c0, c1):
            nc.scalar.activation(yc[:, c0:c1], y[:].indirect(entries(cen_t, c0, c1)), ACT.Copy)

        def neighbours(dst, rows, d, c0, c1, other, op):
            nc.vector.tensor_tensor(dst, rows[:].indirect(entries(pos_t[d], c0, c1)), other, op)

        def sigmoid(pre, name):
            gate = sbuf(V, F32, name)
            nc.scalar.activation(gate[:], pre[:], ACT.Sigmoid)
            return gate

        def sum_turned(msgs, number):
            width = msgs[0].shape[1]
            turned = bank(number, width)
            for d, msg in enumerate(msgs):
                for c0 in range(0, width, P):
                    nc.tensor.matmul(
                        turned[:, c0 : c0 + P], lhsT=msg[:, c0 : c0 + P], rhs=identity[:],
                        is_transpose=True, start=(d == 0 and c0 == 0), stop=(d == 1 and c0 == width - P),
                    )
            return turned

        def relu_turned(turned, name):
            part = sbuf(turned.shape[1], F32, name)
            nc.scalar.activation(part[:], turned[:], ACT.Relu)
            return part

        def turn_back_and_store(part, number, block, v0, name):
            width = part.shape[1]
            back = bank(number, width)
            for c0 in range(0, width, P):
                nc.tensor.transpose(back[:, c0 : c0 + P], part[:, c0 : c0 + P], identity[:])
            res = sbuf(width, F32, name)
            nc.scalar.copy(res[:], back[:])
            nc.sync.dma_start(out[block * P : (block + 1) * P, v0 : v0 + width], res[:])

        y0 = sbuf(S, F32, "y0")
        e0 = sbuf(S, F32, "e0")
        yc0 = sbuf(V, F32, "yc0")
        for i, piece in enumerate(pieces):
            product(block_of(w10_q), y0, piece[2], piece[3], i, nc.scalar.copy)
        for q in range(4):
            product(block_of(w20_q), e0, q * QUARTER, (q + 1) * QUARTER, (5 + q) % 8, nc.vector.tensor_copy if q > 0 else nc.scalar.copy)
            if q == 0:
                centres(yc0, y0, 0, V)
        h0 = sbuf(S, F32, "h0")
        product(block_of(w3_q, 0), h0, 0, P, 1, nc.vector.tensor_copy)
        w21_bf = round_weight(nc.vector.tensor_copy, w21_raw[:], "w21_bf")

        pre00 = sbuf(V, F32, "pre00")
        pre01 = sbuf(V, F32, "pre01")
        neighbours(pre00[:], e0, 0, 0, V, yc0[:], ALU.add)
        w21_q = quantize(w21_bf, (P,), "w21")
        neighbours(pre01[:], e0, 1, 0, V, yc0[:], ALU.add)

        for number, c0, c1 in ((2, P, QUARTER), (3, QUARTER, HALF), (4, HALF, S)):
            product(block_of(w3_q, 0), h0, c0, c1, number, nc.scalar.copy)
        y1 = sbuf(S, F32, "y1")
        product(block_of(w11_q), y1, 0, HALF, 5, nc.scalar.copy)
        gate00 = sigmoid(pre00, "gate00")
        product(block_of(w11_q), y1, HALF, S, 6, nc.scalar.copy)
        e1 = sbuf(S, F32, "e1")
        product(block_of(w21_q), e1, 0, HALF, 7, nc.scalar.copy)
        gate01 = sigmoid(pre01, "gate01")
        product(block_of(w21_q), e1, HALF, S, 5, nc.scalar.copy)
        msg00 = sbuf(V, F32, "msg00")
        msg01 = sbuf(V, F32, "msg01")
        neighbours(msg00[:], h0, 0, 0, V, gate00[:], ALU.mult)
        neighbours(msg01[:], h0, 1, 0, V, gate01[:], ALU.mult)

        yc1 = sbuf(V, F32, "yc1")
        pre10 = sbuf(V, F32, "pre10")
        pre11 = sbuf(V, F32, "pre11")
        sides = [(0, SIDE), (SIDE, V)]
        for c0, c1 in sides:
            centres(yc1, y1, c0, c1)
            neighbours(pre10[:, c0:c1], e1, 0, c0, c1, yc1[:, c0:c1], ALU.add)
        neighbours(pre11[:], e1, 1, 0, V, yc1[:], ALU.add)
        h1 = product_in_halves(block_of(w3_q, 1), "h1", (6, 7))
        gate10 = sigmoid(pre10, "gate10")
        turned = [sum_turned([msg00[:, c0:c1], msg01[:, c0:c1]], 5 + i) for i, (c0, c1) in enumerate(sides)]
        relus = [relu_turned(part, "relu%d" % i) for i, part in enumerate(turned)]
        gate11 = sigmoid(pre11, "gate11")
        fetched = sbuf(SIDE, F32, "fetched")
        nc.scalar.activation(fetched[:], h1[:].indirect(entries(pos_t[1], SIDE, V)), ACT.Copy)
        for i, (c0, c1) in enumerate(sides):
            turn_back_and_store(relus[i], 1 + i, 0, c0, "res0_%d" % i)

        msg10 = sbuf(V, F32, "msg10")
        msg11 = sbuf(V, F32, "msg11")
        neighbours(msg10[:], h1, 0, 0, V, gate10[:], ALU.mult)
        neighbours(msg11[:, :SIDE], h1, 1, 0, SIDE, gate11[:, :SIDE], ALU.mult)
        nc.vector.tensor_tensor(msg11[:, SIDE:], fetched[:], gate11[:, SIDE:], ALU.mult)
        totals = []
        for i, (c0, c1) in enumerate(sides):
            total = sbuf(SIDE, F32, "total%d" % i, ("h1", "total1")[i])
            nc.vector.tensor_tensor(total[:], msg10[:, c0:c1], msg11[:, c0:c1], ALU.add)
            totals.append(total)
        for i, (c0, c1) in enumerate(sides):
            res = sbuf(SIDE, F32, "res1_%d" % i)
            nc.vector.tensor_scalar_max(res[:], totals[i][:], 0.0)
            nc.sync.dma_start(out[P:N, c0:c1], res[:])
